import numpy as np
import ml_dtypes


def mxq(x, axis, fmt="e4m3"):
    dtype, down = {"e4m3": (ml_dtypes.float8_e4m3fn, 7), "e5m2": (ml_dtypes.float8_e5m2, 14)}[fmt]
    v = np.moveaxis(np.asarray(x, np.float32).astype(ml_dtypes.bfloat16).astype(np.float64), axis, -1)
    blocks = v.reshape(v.shape[:-1] + (-1, 32))
    amax = np.abs(blocks).max(-1, keepdims=True)
    byte = np.maximum(np.where(amax > 0, np.frexp(amax)[1] - 1 + 127, 0) - down, 1)
    scale = np.exp2(byte - 127.0)
    codes = (blocks / scale).astype(np.float32).astype(dtype).astype(np.float64)
    return np.moveaxis((codes * scale).reshape(v.shape), -1, axis)


WIDE = False


def mx_kscale(k):
    if not WIDE:
        return np.ones(k)
    levels = np.array([24, -24, 12, -12, 0])
    if k % 512:
        return np.exp2(np.random.permutation(np.resize(levels, k // 32))).repeat(32)
    a = np.empty((k // 512, 16))
    for p in range(k // 512):
        a[p, :8] = np.random.permutation(np.resize(levels, 8))
        for g in range(8):
            far = levels[np.abs(levels - a[p, g]) >= 10]
            a[p, g + 8] = far[np.random.randint(len(far))]
    return np.exp2(a.ravel()).repeat(32)


def f64(x):
    return np.asarray(x).astype(np.float64)


def striped(idx):
    return np.tile(idx.reshape(-1, 16).T, (8, 1)).astype(np.uint16)


def unstriped(offs):
    return offs[:16].T.reshape(-1).astype(np.int64)


E2M1 = np.array([0.0, 0.5, 1.0, 1.5, 2.0, 3.0, 4.0, 6.0, -0.0, -0.5, -1.0, -1.5, -2.0, -3.0, -4.0, -6.0])


def pack_weight(w, fmt):
    k, n = w.shape
    w = f64(np.asarray(w, np.float32).astype(ml_dtypes.bfloat16)).reshape(k // 32, 32, n)
    amax = np.abs(w).max(1)
    if fmt == "e4m3":
        byte = np.frexp(amax)[1] - 1 + 127 - 7
    else:
        mant, ex = np.frexp(amax / 6.0)
        byte = np.where(mant > 0.5, ex, ex - 1) + 127
    byte = np.clip(np.where(amax > 0, byte, 1), 1, 254)
    scaled = (w * np.exp2(127.0 - byte)[:, None, :]).reshape(k, n).astype(np.float32)
    by_word = np.ascontiguousarray(scaled.reshape(k // 512, 128, 4, n).transpose(0, 1, 3, 2))
    if fmt == "e4m3":
        words = by_word.astype(ml_dtypes.float8_e4m3fn).view(np.uint8)
    else:
        c = by_word.astype(ml_dtypes.float4_e2m1fn).view(np.uint8) & 0xF
        words = (c[..., 0::2] | (c[..., 1::2] << 4)).reshape(k // 512, 128, 2 * n)
    return np.ascontiguousarray(words), np.ascontiguousarray(byte.astype(np.uint8).reshape(k // 512, 16, n))


def unpack_weight(words, scales, fmt):
    g, _, n = scales.shape
    words = np.ascontiguousarray(words).reshape(g, 128, n, -1)
    if fmt == "e4m3":
        vals = words.view(ml_dtypes.float8_e4m3fn).astype(np.float64)
    else:
        nib = np.empty((g, 128, n, 4), np.uint8)
        nib[..., 0::2] = words & 0xF
        nib[..., 1::2] = words >> 4
        vals = E2M1[nib]
    vals = vals * np.repeat(np.exp2(scales.astype(np.float64) - 127.0), 8, axis=1)[..., None]
    return vals.transpose(0, 1, 3, 2).reshape(g * 512, n)


K, L, R, N, T, J = 512, 512, 512, 512, 2048, 1024


def setup_inputs():
    n = np.random.standard_normal
    s = mx_kscale(K)[:, None]
    s2 = mx_kscale(L)[:, None]
    u = mx_kscale(R)[:, None]
    p_tab = pack_weight(n((K, T)) * s, "e4m3")
    p_tab2 = pack_weight(n((L, T)) * s2, "e4m3")
    p_wer = pack_weight(n((K, R)) / np.sqrt(K) / s * u.T, "e4m3")
    p_wei = pack_weight(n((K, R)) / np.sqrt(K) / s * u.T, "e4m3")
    p_nr = pack_weight(n((R, N)) / np.sqrt(R) / u, "e4m3")
    p_ni = pack_weight(n((R, N)) / np.sqrt(R) / u, "e2m1")
    return {
        "tab_words": p_tab[0],
        "tab_scales": p_tab[1],
        "tab2_words": p_tab2[0],
        "tab2_scales": p_tab2[1],
        "wer_words": p_wer[0],
        "wer_scales": p_wer[1],
        "wei_words": p_wei[0],
        "wei_scales": p_wei[1],
        "wrr": (n((L, R)) / np.sqrt(L) / s2).astype(np.float32),
        "wri": (n((L, R)) / np.sqrt(L) / s2).astype(np.float32),
        "nr_words": p_nr[0],
        "nr_scales": p_nr[1],
        "ni_words": p_ni[0],
        "ni_scales": p_ni[1],
        "offs": striped(np.random.permutation(T)[:J]),
        "offs2": striped(np.random.permutation(T)[:J]),
    }


def reference(tab_words, tab_scales, tab2_words, tab2_scales, wer_words, wer_scales, wei_words, wei_scales, wrr, wri, nr_words, nr_scales, ni_words, ni_scales, offs, offs2):
    idx = unstriped(offs)
    idx2 = unstriped(offs2)
    tab_ = unpack_weight(tab_words, tab_scales, "e4m3")[:, idx]
    tab2_ = unpack_weight(tab2_words, tab2_scales, "e4m3")[:, idx2]
    wer_ = unpack_weight(wer_words, wer_scales, "e4m3")
    aer = wer_.T @ tab_
    wei_ = unpack_weight(wei_words, wei_scales, "e4m3")
    aei = wei_.T @ tab_
    wrr_ = mxq(f64(wrr), 0, "e4m3")
    arr = wrr_.T @ tab2_
    wri_ = mxq(f64(wri), 0, "e4m3")
    ari = wri_.T @ tab2_
    hr = aer * arr - aei * ari
    hi = aer * ari + aei * arr
    hr_ = mxq(hr, 0, "e4m3")
    hi_ = mxq(hi, 0, "e4m3")
    nr_ = unpack_weight(nr_words, nr_scales, "e4m3")
    ni_ = unpack_weight(ni_words, ni_scales, "e2m1")
    y = nr_.T @ hr_ + ni_.T @ hi_
    return y

@@ -1,0 +1,185 @@
+from contextlib import ExitStack
+
+import concourse.mybir as mybir
+
+K, L, R, N, T, J = 512, 512, 512, 512, 2048, 1024
+FLOPS = 2 * J * (2 * K * R + 2 * L * R + 2 * R * N)
+
+F32 = mybir.dt.float32
+BF16 = mybir.dt.bfloat16
+I32 = mybir.dt.int32
+U32 = mybir.dt.uint32
+U16 = mybir.dt.uint16
+U8 = mybir.dt.uint8
+FP8X4 = mybir.dt.float8_e4m3fn_x4
+FP4X4 = mybir.dt.float4_e2m1fn_x4
+MULT = mybir.AluOpType.mult
+ADD = mybir.AluOpType.add
+
+P = 128
+PACK = 4
+JB = 128
+BLOCKS = J // JB
+PIECE = 256
+AL = 64
+
+
+def tile_list_ckg_none_kernel(
+    tc, tab_words, tab_scales, tab2_words, tab2_scales, wer_words, wer_scales, wei_words, wei_scales,
+    wrr, wri, nr_words, nr_scales, ni_words, ni_scales, offs, offs2, out,
+):
+    nc = tc.nc
+    with ExitStack() as ctx:
+        keep = ctx.enter_context(tc.tile_pool(name="keep", bufs=1))
+        ring = ctx.enter_context(tc.tile_pool(name="ring", bufs=2))
+        psum1 = ctx.enter_context(tc.psum_pool(name="psum1", bufs=1))
+        psum2 = ctx.enter_context(tc.psum_pool(name="psum2", bufs=2))
+
+        list_e = keep.tile([P, J // 16], U16, name="list_e")
+        list_r = keep.tile([P, J // 16], U16, name="list_r")
+        tab_e = keep.tile([P, T], I32, name="tab_e", align_bytes=AL)
+        tab_r = keep.tile([P, T], I32, name="tab_r", align_bytes=AL)
+        tab_e_sc = keep.tile([P, T // 4], I32, name="tab_e_sc", align_bytes=AL)
+        tab_r_sc = keep.tile([P, T // 4], I32, name="tab_r_sc", align_bytes=AL)
+        we_raw = keep.tile([P, 2, R], I32, name="we_raw", align_bytes=AL)
+        we_sc_raw = keep.tile([P, R // 4], I32, name="we_sc_raw", align_bytes=AL)
+        we = keep.tile([P, 2, R], I32, name="we", align_bytes=AL)
+        we_sc = keep.tile([P, R], U8, name="we_sc", align_bytes=AL)
+        wr_raw = [keep.tile([P, PACK, R], F32, name="wr_raw%d" % c, align_bytes=AL) for c in range(2)]
+        wr_bf = [keep.tile([P, R * PACK], BF16, name="wr_bf%d" % c, align_bytes=AL) for c in range(2)]
+        wr = keep.tile([P, 2, R], U32, name="wr", align_bytes=AL)
+        wr_sc = keep.tile([P, 2, R], U8, name="wr_sc", align_bytes=AL)
+        nr = keep.tile([P, N], I32, name="nr", align_bytes=AL)
+        ni = keep.tile([P, N // 2], I32, name="ni", align_bytes=AL)
+        n_sc = keep.tile([P, N // 4], I32, name="n_sc", align_bytes=AL)
+        ve = keep.tile([P, J], U32, name="ve", align_bytes=AL)
+        vr = keep.tile([P, J], U32, name="vr", align_bytes=AL)
+        ve_sc = keep.tile([P, J], U8, name="ve_sc", align_bytes=AL)
+        vr_sc = keep.tile([P, J], U8, name="vr_sc", align_bytes=AL)
+
+        def words(ap):
+            return ap[0].rearrange("p n i -> p (n i)").bitcast(I32)
+
+        def load_scales(queue, plane, scales, first):
+            rows = scales[0].bitcast(I32).rearrange("(q r) c -> r q c", r=4)
+            for r in range(4):
+                queue.dma_start(out=plane[first + r : P : 32, :], in_=rows[r])
+
+        for plane in (tab_e_sc, tab_r_sc, n_sc):
+            nc.vector.memset(plane[:], 0)
+        nc.gpsimd.memset(we_sc_raw[:], 0)
+        nc.sync.dma_start(list_e[:], offs)
+        nc.sync.dma_start(list_r[:], offs2)
+        load_scales(nc.scalar, tab_e_sc, tab_scales, 0)
+        load_scales(nc.scalar, tab_r_sc, tab2_scales, 0)
+        load_scales(nc.gpsimd, we_sc_raw, wer_scales, 0)
+        load_scales(nc.gpsimd, we_sc_raw, wei_scales, 4)
+        nc.sync.dma_start(out=tab_e[:], in_=words(tab_words))
+        nc.sync.dma_start(out=wr_raw[0][:], in_=wrr.rearrange("(p i) r -> p i r", i=PACK))
+        nc.sync.dma_start(out=wr_raw[1][:], in_=wri.rearrange("(p i) r -> p i r", i=PACK))
+        nc.sync.dma_start(out=we_raw[:, 0, :], in_=words(wer_words))
+        nc.sync.dma_start(out=we_raw[:, 1, :], in_=words(wei_words))
+        nc.sync.dma_start(out=tab_r[:], in_=words(tab2_words))
+        nc.sync.dma_start(out=nr[:], in_=words(nr_words))
+        nc.sync.dma_start(out=ni[:], in_=ni_words[0].bitcast(I32))
+        load_scales(nc.sync, n_sc, ni_scales, 0)
+        load_scales(nc.sync, n_sc, nr_scales, 4)
+
+        def gather(dst, window, offsets, piece):
+            nc.vector.tensor_copy(
+                dst[:, piece * PIECE : (piece + 1) * PIECE],
+                window.indirect(offsets[:, piece * PIECE // 16 : (piece + 1) * PIECE // 16]),
+            )
+
+        def gather_piece(piece):
+            gather(ve_sc, tab_e_sc[:].bitcast(U8), list_e, piece)
+            gather(vr_sc, tab_r_sc[:].bitcast(U8), list_r, piece)
+            gather(ve, tab_e[:].bitcast(U32), list_e, piece)
+            gather(vr, tab_r[:].bitcast(U32), list_r, piece)
+
+        for c in range(2):
+            nc.scalar.copy(
+                out=wr_bf[c][:].rearrange("p (t m i) -> p m i t", t=PACK, i=PACK),
+                in_=wr_raw[c][:].rearrange("p i (m t) -> p m i t", t=PACK),
+            )
+            nc.vector.quantize_mx(out=wr[:, c, :].bitcast(FP8X4), scales=wr_sc[:, c, :], in_=wr_bf[c][:])
+        nc.vector.tensor_copy(
+            out=we[:].rearrange("p c (t m) -> p c m t", t=PACK),
+            in_=we_raw[:].rearrange("p c (m t) -> p c m t", t=PACK),
+        )
+        nc.vector.tensor_copy(
+            out=we_sc[:].rearrange("p (t m) -> p m t", t=PACK),
+            in_=we_sc_raw[:].bitcast(U8).rearrange("p (m t) -> p m t", t=PACK),
+        )
+        n_sc8 = n_sc[:].bitcast(U8)
+        ni8 = ni[:].bitcast(U8)
+
+        def project(bank, codes, plane, moving, moving_sc, b):
+            cols = slice(b * JB, (b + 1) * JB)
+            for t in range(PACK):
+                m = slice(t * P, (t + 1) * P)
+                nc.tensor.matmul_mx(
+                    out=bank[:, t, :], lhsT=codes[:, m].bitcast(FP8X4), lhsT_scale=plane[:, m],
+                    rhs=moving[:, cols].bitcast(FP8X4), rhs_scale=moving_sc[:, cols], start=True, stop=True,
+                )
+
+        def products(b):
+            aer = psum1.tile([P, PACK, JB], F32, name="aer")
+            aei = psum1.tile([P, PACK, JB], F32, name="aei")
+            arr = psum2.tile([P, PACK, JB], F32, name="arr")
+            ari = psum2.tile([P, PACK, JB], F32, name="ari")
+            project(aer, we[:, 0, :], we_sc[:, :], ve, ve_sc, b)
+            project(aei, we[:, 1, :], we_sc[4:P, :], ve, ve_sc, b)
+            project(arr, wr[:, 0, :], wr_sc[:, 0, :], vr, vr_sc, b)
+            project(ari, wr[:, 1, :], wr_sc[:, 1, :], vr, vr_sc, b)
+            ae = ring.tile([P, 2, JB, PACK], F32, name="ae", bufs=3)
+            nc.scalar.copy(out=ae[:, 0], in_=aer[:].rearrange("p t j -> p j t"))
+            nc.scalar.copy(out=ae[:, 1], in_=aei[:].rearrange("p t j -> p j t"))
+            by_arr = ring.tile([P, 2, JB, PACK], F32, name="by_arr")
+            by_ari = ring.tile([P, 2, JB, PACK], F32, name="by_ari")
+            arr_jt = arr[:].rearrange("p t j -> p j t")
+            ari_jt = ari[:].rearrange("p t j -> p j t")
+            nc.vector.tensor_tensor(by_arr[:], arr_jt.unsqueeze(1).to_broadcast([P, 2, JB, PACK]), ae[:], MULT)
+            nc.vector.scalar_tensor_tensor(by_ari[:, 0], ari_jt, -1.0, ae[:, 1], MULT, MULT)
+            nc.vector.tensor_tensor(by_ari[:, 1], ari_jt, ae[:, 0], MULT)
+            return by_arr, by_ari
+
+        def combine(b, terms):
+            by_arr, by_ari = terms
+            h = keep.tile([P, 2 * JB * PACK], BF16, name="h", align_bytes=AL)
+            engine = nc.vector if b == BLOCKS - 1 else nc.gpsimd
+            engine.tensor_tensor(
+                h[:], by_arr[:].rearrange("p c j t -> p (c j t)"), by_ari[:].rearrange("p c j t -> p (c j t)"), ADD
+            )
+            return h
+
+        def score(b, h):
+            hq = ring.tile([P, 2 * JB], U32, name="hq", align_bytes=AL)
+            hq_sc = ring.tile([P, 2 * JB], U8, name="hq_sc", align_bytes=AL)
+            nc.vector.quantize_mx(out=hq[:].bitcast(FP8X4), scales=hq_sc[:], in_=h[:])
+            y = psum2.tile([P, N // P, JB], F32, name="y")
+            for g in range(N // P):
+                m = slice(g * P, (g + 1) * P)
+                nc.tensor.matmul_mx(
+                    out=y[:, g, :], lhsT=nr[:, m].bitcast(FP8X4), lhsT_scale=n_sc8[4:P, m],
+                    rhs=hq[:, 0:JB].bitcast(FP8X4), rhs_scale=hq_sc[:, 0:JB], start=True, stop=False,
+                )
+                nc.tensor.matmul_mx(
+                    out=y[:, g, :], lhsT=ni8[:, 2 * g * P : 2 * (g + 1) * P].bitcast(FP4X4), lhsT_scale=n_sc8[:, m],
+                    rhs=hq[:, JB : 2 * JB].bitcast(FP8X4), rhs_scale=hq_sc[:, JB : 2 * JB], start=False, stop=True,
+                )
+            y_sb = ring.tile([P, N // P, JB], F32, name="y_sb", bufs=3)
+            nc.scalar.copy(out=y_sb[:], in_=y[:])
+            nc.sync.dma_start(
+                out=out[:, b * JB : (b + 1) * JB].rearrange("(g p) j -> p g j", p=P), in_=y_sb[:]
+            )
+
+        h = None
+        for b in range(BLOCKS):
+            if (b * JB) % PIECE == 0:
+                gather_piece(b * JB // PIECE)
+            terms = products(b)
+            if b > 0:
+                score(b - 1, h)
+            h = combine(b, terms)
+        score(BLOCKS - 1, h)

@@ -65,44 +65,40 @@ def tile_list_ckg_none_kernel(
             for r in range(4):
                 queue.dma_start(out=plane[first + r : P : 32, :], in_=rows[r])
 
-        for plane in (tab_e_sc, tab_r_sc, n_sc):
+        for plane in (tab_e_sc, tab_r_sc, we_sc_raw, n_sc):
             nc.vector.memset(plane[:], 0)
-        nc.gpsimd.memset(we_sc_raw[:], 0)
+        nc.scalar.dma_start(out=tab_e[:], in_=words(tab_words))
+        nc.gpsimd.dma_start(out=wr_raw[0][:], in_=wrr.rearrange("(p i) r -> p i r", i=PACK))
+        nc.gpsimd.dma_start(out=wr_raw[1][:], in_=wri.rearrange("(p i) r -> p i r", i=PACK))
+        nc.gpsimd.dma_start(out=we_raw[:, 0, :], in_=words(wer_words))
+        nc.gpsimd.dma_start(out=we_raw[:, 1, :], in_=words(wei_words))
+        nc.gpsimd.dma_start(out=tab_r[:], in_=words(tab2_words))
+        nc.gpsimd.dma_start(out=nr[:], in_=words(nr_words))
+        nc.gpsimd.dma_start(out=ni[:], in_=ni_words[0].bitcast(I32))
         nc.sync.dma_start(list_e[:], offs)
+        load_scales(nc.sync, tab_e_sc, tab_scales, 0)
         nc.sync.dma_start(list_r[:], offs2)
-        load_scales(nc.scalar, tab_e_sc, tab_scales, 0)
-        load_scales(nc.scalar, tab_r_sc, tab2_scales, 0)
-        load_scales(nc.gpsimd, we_sc_raw, wer_scales, 0)
-        load_scales(nc.gpsimd, we_sc_raw, wei_scales, 4)
-        nc.sync.dma_start(out=tab_e[:], in_=words(tab_words))
-        nc.sync.dma_start(out=wr_raw[0][:], in_=wrr.rearrange("(p i) r -> p i r", i=PACK))
-        nc.sync.dma_start(out=wr_raw[1][:], in_=wri.rearrange("(p i) r -> p i r", i=PACK))
-        nc.sync.dma_start(out=we_raw[:, 0, :], in_=words(wer_words))
-        nc.sync.dma_start(out=we_raw[:, 1, :], in_=words(wei_words))
-        nc.sync.dma_start(out=tab_r[:], in_=words(tab2_words))
-        nc.sync.dma_start(out=nr[:], in_=words(nr_words))
-        nc.sync.dma_start(out=ni[:], in_=ni_words[0].bitcast(I32))
+        load_scales(nc.sync, tab_r_sc, tab2_scales, 0)
+        load_scales(nc.sync, we_sc_raw, wer_scales, 0)
+        load_scales(nc.sync, we_sc_raw, wei_scales, 4)
         load_scales(nc.sync, n_sc, ni_scales, 0)
         load_scales(nc.sync, n_sc, nr_scales, 4)
 
-        def gather(dst, window, offsets, piece):
-            nc.vector.tensor_copy(
-                dst[:, piece * PIECE : (piece + 1) * PIECE],
-                window.indirect(offsets[:, piece * PIECE // 16 : (piece + 1) * PIECE // 16]),
-            )
+        def gather(dst, window, offsets, first, last):
+            nc.vector.tensor_copy(dst[:, first:last], window.indirect(offsets[:, first // 16 : last // 16]))
 
-        def gather_piece(piece):
-            gather(ve_sc, tab_e_sc[:].bitcast(U8), list_e, piece)
-            gather(vr_sc, tab_r_sc[:].bitcast(U8), list_r, piece)
-            gather(ve, tab_e[:].bitcast(U32), list_e, piece)
-            gather(vr, tab_r[:].bitcast(U32), list_r, piece)
+        gather(ve_sc, tab_e_sc[:].bitcast(U8), list_e, 0, J)
+        gather(ve, tab_e[:].bitcast(U32), list_e, 0, J)
+        gather(vr_sc, tab_r_sc[:].bitcast(U8), list_r, 0, J)
 
-        for c in range(2):
+        def quantize_weight(c):
             nc.scalar.copy(
                 out=wr_bf[c][:].rearrange("p (t m i) -> p m i t", t=PACK, i=PACK),
                 in_=wr_raw[c][:].rearrange("p i (m t) -> p m i t", t=PACK),
             )
             nc.vector.quantize_mx(out=wr[:, c, :].bitcast(FP8X4), scales=wr_sc[:, c, :], in_=wr_bf[c][:])
+
+        quantize_weight(0)
         nc.vector.tensor_copy(
             out=we[:].rearrange("p c (t m) -> p c m t", t=PACK),
             in_=we_raw[:].rearrange("p c (m t) -> p c m t", t=PACK),
@@ -111,6 +107,9 @@ def tile_list_ckg_none_kernel(
             out=we_sc[:].rearrange("p (t m) -> p m t", t=PACK),
             in_=we_sc_raw[:].bitcast(U8).rearrange("p (m t) -> p m t", t=PACK),
         )
+        quantize_weight(1)
+        for first in range(0, J - PIECE, PIECE):
+            gather(vr, tab_r[:].bitcast(U32), list_r, first, first + PIECE)
         n_sc8 = n_sc[:].bitcast(U8)
         ni8 = ni[:].bitcast(U8)
 
@@ -124,10 +123,10 @@ def tile_list_ckg_none_kernel(
                 )
 
         def products(b):
-            aer = psum1.tile([P, PACK, JB], F32, name="aer")
-            aei = psum1.tile([P, PACK, JB], F32, name="aei")
-            arr = psum2.tile([P, PACK, JB], F32, name="arr")
-            ari = psum2.tile([P, PACK, JB], F32, name="ari")
+            aer = psum1.tile([P, PACK, JB], F32, name="aer", tag="aer")
+            aei = psum1.tile([P, PACK, JB], F32, name="aei", tag="aei")
+            arr = psum2.tile([P, PACK, JB], F32, name="arr", tag="arr")
+            ari = psum2.tile([P, PACK, JB], F32, name="ari", tag="ari")
             project(aer, we[:, 0, :], we_sc[:, :], ve, ve_sc, b)
             project(aei, we[:, 1, :], we_sc[4:P, :], ve, ve_sc, b)
             project(arr, wr[:, 0, :], wr_sc[:, 0, :], vr, vr_sc, b)
@@ -135,8 +134,8 @@ def tile_list_ckg_none_kernel(
             ae = ring.tile([P, 2, JB, PACK], F32, name="ae", bufs=3)
             nc.scalar.copy(out=ae[:, 0], in_=aer[:].rearrange("p t j -> p j t"))
             nc.scalar.copy(out=ae[:, 1], in_=aei[:].rearrange("p t j -> p j t"))
-            by_arr = ring.tile([P, 2, JB, PACK], F32, name="by_arr")
-            by_ari = ring.tile([P, 2, JB, PACK], F32, name="by_ari")
+            by_arr = ring.tile([P, 2, JB, PACK], F32, name="by_arr", bufs=3)
+            by_ari = ring.tile([P, 2, JB, PACK], F32, name="by_ari", bufs=3)
             arr_jt = arr[:].rearrange("p t j -> p j t")
             ari_jt = ari[:].rearrange("p t j -> p j t")
             nc.vector.tensor_tensor(by_arr[:], arr_jt.unsqueeze(1).to_broadcast([P, 2, JB, PACK]), ae[:], MULT)
@@ -144,14 +143,30 @@ def tile_list_ckg_none_kernel(
             nc.vector.tensor_tensor(by_ari[:, 1], ari_jt, ae[:, 0], MULT)
             return by_arr, by_ari
 
-        def combine(b, terms):
+        def flat(terms):
+            return terms.rearrange("p c j t -> p (c j t)")
+
+        def combine(terms):
             by_arr, by_ari = terms
-            h = keep.tile([P, 2 * JB * PACK], BF16, name="h", align_bytes=AL)
-            engine = nc.vector if b == BLOCKS - 1 else nc.gpsimd
-            engine.tensor_tensor(
-                h[:], by_arr[:].rearrange("p c j t -> p (c j t)"), by_ari[:].rearrange("p c j t -> p (c j t)"), ADD
-            )
+            h = ring.tile([P, 2 * JB * PACK], BF16, name="h", align_bytes=AL, bufs=3)
+            nc.gpsimd.tensor_tensor(h[:], flat(by_arr[:]), flat(by_ari[:]), ADD)
             return h
+
+        def score_pass(y, g, part, hq, hq_sc):
+            m = slice(g * P, (g + 1) * P)
+            cols = slice(part * JB, (part + 1) * JB)
+            if part == 0:
+                lhsT, lhsT_scale = nr[:, m].bitcast(FP8X4), n_sc8[4:P, m]
+            else:
+                lhsT, lhsT_scale = ni8[:, 2 * g * P : 2 * (g + 1) * P].bitcast(FP4X4), n_sc8[:, m]
+            nc.tensor.matmul_mx(
+                out=y, lhsT=lhsT, lhsT_scale=lhsT_scale, rhs=hq[:, cols].bitcast(FP8X4), rhs_scale=hq_sc[:, cols],
+                start=(part == 0), stop=(part == 1),
+            )
+
+        def store(b, y_sb, groups):
+            rows = out[:, b * JB : (b + 1) * JB].rearrange("(g p) j -> p g j", p=P)
+            nc.sync.dma_start(out=rows[:, groups, :], in_=y_sb[:, groups, :])
 
         def score(b, h):
             hq = ring.tile([P, 2 * JB], U32, name="hq", align_bytes=AL)
@@ -159,27 +174,54 @@ def tile_list_ckg_none_kernel(
             nc.vector.quantize_mx(out=hq[:].bitcast(FP8X4), scales=hq_sc[:], in_=h[:])
             y = psum2.tile([P, N // P, JB], F32, name="y")
             for g in range(N // P):
-                m = slice(g * P, (g + 1) * P)
-                nc.tensor.matmul_mx(
-                    out=y[:, g, :], lhsT=nr[:, m].bitcast(FP8X4), lhsT_scale=n_sc8[4:P, m],
-                    rhs=hq[:, 0:JB].bitcast(FP8X4), rhs_scale=hq_sc[:, 0:JB], start=True, stop=False,
-                )
-                nc.tensor.matmul_mx(
-                    out=y[:, g, :], lhsT=ni8[:, 2 * g * P : 2 * (g + 1) * P].bitcast(FP4X4), lhsT_scale=n_sc8[:, m],
-                    rhs=hq[:, JB : 2 * JB].bitcast(FP8X4), rhs_scale=hq_sc[:, JB : 2 * JB], start=False, stop=True,
-                )
+                for part in range(2):
+                    score_pass(y[:, g, :], g, part, hq, hq_sc)
             y_sb = ring.tile([P, N // P, JB], F32, name="y_sb", bufs=3)
             nc.scalar.copy(out=y_sb[:], in_=y[:])
-            nc.sync.dma_start(
-                out=out[:, b * JB : (b + 1) * JB].rearrange("(g p) j -> p g j", p=P), in_=y_sb[:]
-            )
+            store(b, y_sb, slice(0, N // P))
 
-        h = None
+        def last_block(b, terms):
+            by_arr, by_ari = terms
+            h = ring.tile([P, 2 * JB * PACK], BF16, name="h", align_bytes=AL, bufs=3)
+            hq = ring.tile([P, 2 * JB], U32, name="hq", align_bytes=AL)
+            hq_sc = ring.tile([P, 2 * JB], U8, name="hq_sc", align_bytes=AL)
+            width = JB * PACK
+            for part in range(2):
+                cols = slice(part * width, (part + 1) * width)
+                nc.vector.tensor_tensor(h[:, cols], flat(by_arr[:])[:, cols], flat(by_ari[:])[:, cols], ADD)
+            for part in range(2):
+                nc.vector.quantize_mx(
+                    out=hq[:, part * JB : (part + 1) * JB].bitcast(FP8X4),
+                    scales=hq_sc[:, part * JB : (part + 1) * JB],
+                    in_=h[:, part * width : (part + 1) * width],
+                )
+            banks = [
+                psum1.tile([P, JB], F32, name="y0", tag="aer"),
+                psum1.tile([P, JB], F32, name="y1", tag="aei"),
+                psum2.tile([P, JB], F32, name="y2", tag="arr"),
+                psum2.tile([P, JB], F32, name="y3", tag="ari"),
+            ]
+            for part in range(2):
+                for g in range(N // P):
+                    score_pass(banks[g][:], g, part, hq, hq_sc)
+            y_sb = ring.tile([P, N // P, JB], F32, name="y_sb", bufs=3)
+            for g in range(N // P):
+                if g % 2 == 0:
+                    nc.scalar.copy(out=y_sb[:, g, :], in_=banks[g][:])
+                else:
+                    nc.vector.tensor_copy(out=y_sb[:, g, :], in_=banks[g][:])
+                    store(b, y_sb, slice(g - 1, g + 1))
+
+        h = {}
+        after = {b: [b - 2] for b in range(2, BLOCKS - 2)}
+        after[BLOCKS - 2] = [BLOCKS - 4, BLOCKS - 3]
+        after[BLOCKS - 1] = [BLOCKS - 2]
         for b in range(BLOCKS):
-            if (b * JB) % PIECE == 0:
-                gather_piece(b * JB // PIECE)
             terms = products(b)
-            if b > 0:
-                score(b - 1, h)
-            h = combine(b, terms)
-        score(BLOCKS - 1, h)
+            if b == 0:
+                gather(vr, tab_r[:].bitcast(U32), list_r, J - PIECE, J)
+            for done in after.get(b, []):
+                score(done, h[done])
+            if b < BLOCKS - 1:
+                h[b] = combine(terms)
+        last_block(BLOCKS - 1, terms)

@@ -60,14 +60,14 @@ def tile_list_ckg_none_kernel(
         def words(ap):
             return ap[0].rearrange("p n i -> p (n i)").bitcast(I32)
 
-        def load_scales(queue, plane, scales, first):
+        def load_scales(queues, plane, scales, first):
             rows = scales[0].bitcast(I32).rearrange("(q r) c -> r q c", r=4)
             for r in range(4):
-                queue.dma_start(out=plane[first + r : P : 32, :], in_=rows[r])
+                queues[r * len(queues) // 4].dma_start(out=plane[first + r : P : 32, :], in_=rows[r])
 
         for plane in (tab_e_sc, tab_r_sc, we_sc_raw, n_sc):
             nc.vector.memset(plane[:], 0)
-        nc.scalar.dma_start(out=tab_e[:], in_=words(tab_words))
+        nc.gpsimd.dma_start(out=tab_e[:], in_=words(tab_words))
         nc.gpsimd.dma_start(out=wr_raw[0][:], in_=wrr.rearrange("(p i) r -> p i r", i=PACK))
         nc.gpsimd.dma_start(out=wr_raw[1][:], in_=wri.rearrange("(p i) r -> p i r", i=PACK))
         nc.gpsimd.dma_start(out=we_raw[:, 0, :], in_=words(wer_words))
@@ -76,13 +76,13 @@ def tile_list_ckg_none_kernel(
         nc.gpsimd.dma_start(out=nr[:], in_=words(nr_words))
         nc.gpsimd.dma_start(out=ni[:], in_=ni_words[0].bitcast(I32))
         nc.sync.dma_start(list_e[:], offs)
-        load_scales(nc.sync, tab_e_sc, tab_scales, 0)
+        load_scales([nc.scalar, nc.sync], tab_e_sc, tab_scales, 0)
         nc.sync.dma_start(list_r[:], offs2)
-        load_scales(nc.sync, tab_r_sc, tab2_scales, 0)
-        load_scales(nc.sync, we_sc_raw, wer_scales, 0)
-        load_scales(nc.sync, we_sc_raw, wei_scales, 4)
-        load_scales(nc.sync, n_sc, ni_scales, 0)
-        load_scales(nc.sync, n_sc, nr_scales, 4)
+        load_scales([nc.scalar, nc.sync], tab_r_sc, tab2_scales, 0)
+        load_scales([nc.scalar], we_sc_raw, wer_scales, 0)
+        load_scales([nc.sync], we_sc_raw, wei_scales, 4)
+        load_scales([nc.sync], n_sc, ni_scales, 0)
+        load_scales([nc.sync], n_sc, nr_scales, 4)
 
         def gather(dst, window, offsets, first, last):
             nc.vector.tensor_copy(dst[:, first:last], window.indirect(offsets[:, first // 16 : last // 16]))
@@ -169,8 +169,8 @@ def tile_list_ckg_none_kernel(
             nc.sync.dma_start(out=rows[:, groups, :], in_=y_sb[:, groups, :])
 
         def score(b, h):
-            hq = ring.tile([P, 2 * JB], U32, name="hq", align_bytes=AL)
-            hq_sc = ring.tile([P, 2 * JB], U8, name="hq_sc", align_bytes=AL)
+            hq = ring.tile([P, 2 * JB], U32, name="hq", align_bytes=AL, bufs=3)
+            hq_sc = ring.tile([P, 2 * JB], U8, name="hq_sc", align_bytes=AL, bufs=3)
             nc.vector.quantize_mx(out=hq[:].bitcast(FP8X4), scales=hq_sc[:], in_=h[:])
             y = psum2.tile([P, N // P, JB], F32, name="y")
             for g in range(N // P):
@@ -183,8 +183,8 @@ def tile_list_ckg_none_kernel(
         def last_block(b, terms):
             by_arr, by_ari = terms
             h = ring.tile([P, 2 * JB * PACK], BF16, name="h", align_bytes=AL, bufs=3)
-            hq = ring.tile([P, 2 * JB], U32, name="hq", align_bytes=AL)
-            hq_sc = ring.tile([P, 2 * JB], U8, name="hq_sc", align_bytes=AL)
+            hq = ring.tile([P, 2 * JB], U32, name="hq", align_bytes=AL, bufs=3)
+            hq_sc = ring.tile([P, 2 * JB], U8, name="hq_sc", align_bytes=AL, bufs=3)
             width = JB * PACK
             for part in range(2):
                 cols = slice(part * width, (part + 1) * width)
@@ -213,9 +213,8 @@ def tile_list_ckg_none_kernel(
                     store(b, y_sb, slice(g - 1, g + 1))
 
         h = {}
-        after = {b: [b - 2] for b in range(2, BLOCKS - 2)}
-        after[BLOCKS - 2] = [BLOCKS - 4, BLOCKS - 3]
-        after[BLOCKS - 1] = [BLOCKS - 2]
+        after = {b: [b - 2] for b in range(2, BLOCKS - 1)}
+        after[BLOCKS - 1] = [BLOCKS - 3, BLOCKS - 2]
         for b in range(BLOCKS):
             terms = products(b)
             if b == 0:

@@ -51,9 +51,7 @@ def tile_list_ckg_none_kernel(
         wr_sc = keep.tile([P, 2, R], U8, name="wr_sc", align_bytes=AL)
         nr = keep.tile([P, N], I32, name="nr", align_bytes=AL)
         ni = keep.tile([P, N // 2], I32, name="ni", align_bytes=AL)
-        n_sc = keep.tile([P, N // 4], I32, name="n_sc", align_bytes=AL)
         ve = keep.tile([P, J], U32, name="ve", align_bytes=AL)
-        vr = keep.tile([P, J], U32, name="vr", align_bytes=AL)
         ve_sc = keep.tile([P, J], U8, name="ve_sc", align_bytes=AL)
         vr_sc = keep.tile([P, J], U8, name="vr_sc", align_bytes=AL)
 
@@ -65,10 +63,10 @@ def tile_list_ckg_none_kernel(
             for r in range(4):
                 queues[r * len(queues) // 4].dma_start(out=plane[first + r : P : 32, :], in_=rows[r])
 
-        for plane in (tab_e_sc, tab_r_sc, we_sc_raw, n_sc):
+        for plane in (tab_e_sc, tab_r_sc, we_sc_raw):
             nc.vector.memset(plane[:], 0)
-        nc.gpsimd.dma_start(out=tab_e[:], in_=words(tab_words))
         nc.gpsimd.dma_start(out=wr_raw[0][:], in_=wrr.rearrange("(p i) r -> p i r", i=PACK))
+        nc.gpsimd.dma_start(out=tab_e[:], in_=words(tab_words))
         nc.gpsimd.dma_start(out=wr_raw[1][:], in_=wri.rearrange("(p i) r -> p i r", i=PACK))
         nc.gpsimd.dma_start(out=we_raw[:, 0, :], in_=words(wer_words))
         nc.gpsimd.dma_start(out=we_raw[:, 1, :], in_=words(wei_words))
@@ -79,17 +77,23 @@ def tile_list_ckg_none_kernel(
         load_scales([nc.scalar, nc.sync], tab_e_sc, tab_scales, 0)
         nc.sync.dma_start(list_r[:], offs2)
         load_scales([nc.scalar, nc.sync], tab_r_sc, tab2_scales, 0)
-        load_scales([nc.scalar], we_sc_raw, wer_scales, 0)
+        load_scales([nc.sync], we_sc_raw, wer_scales, 0)
         load_scales([nc.sync], we_sc_raw, wei_scales, 4)
-        load_scales([nc.sync], n_sc, ni_scales, 0)
-        load_scales([nc.sync], n_sc, nr_scales, 4)
 
         def gather(dst, window, offsets, first, last):
             nc.vector.tensor_copy(dst[:, first:last], window.indirect(offsets[:, first // 16 : last // 16]))
 
         gather(ve_sc, tab_e_sc[:].bitcast(U8), list_e, 0, J)
-        gather(ve, tab_e[:].bitcast(U32), list_e, 0, J)
         gather(vr_sc, tab_r_sc[:].bitcast(U8), list_r, 0, J)
+        gather(ve, tab_e[:].bitcast(U32), list_e, 0, J)
+
+        vr = {}
+
+        def gather_relation_words(first, last):
+            piece = ring.tile([P, last - first], U32, name="vr_piece", align_bytes=AL)
+            nc.vector.tensor_copy(piece[:], tab_r[:].bitcast(U32).indirect(list_r[:, first // 16 : last // 16]))
+            for b in range(first // JB, last // JB):
+                vr[b] = piece[:, b * JB - first : (b + 1) * JB - first]
 
         def quantize_weight(c):
             nc.scalar.copy(
@@ -107,9 +111,12 @@ def tile_list_ckg_none_kernel(
             out=we_sc[:].rearrange("p (t m) -> p m t", t=PACK),
             in_=we_sc_raw[:].bitcast(U8).rearrange("p (m t) -> p m t", t=PACK),
         )
+        n_sc = we_sc_raw
+        load_scales([nc.sync], n_sc, ni_scales, 0)
+        load_scales([nc.sync], n_sc, nr_scales, 4)
         quantize_weight(1)
-        for first in range(0, J - PIECE, PIECE):
-            gather(vr, tab_r[:].bitcast(U32), list_r, first, first + PIECE)
+        gather_relation_words(0, PIECE)
+        gather_relation_words(PIECE, 2 * PIECE)
         n_sc8 = n_sc[:].bitcast(U8)
         ni8 = ni[:].bitcast(U8)
 
@@ -119,21 +126,25 @@ def tile_list_ckg_none_kernel(
                 m = slice(t * P, (t + 1) * P)
                 nc.tensor.matmul_mx(
                     out=bank[:, t, :], lhsT=codes[:, m].bitcast(FP8X4), lhsT_scale=plane[:, m],
-                    rhs=moving[:, cols].bitcast(FP8X4), rhs_scale=moving_sc[:, cols], start=True, stop=True,
+                    rhs=moving.bitcast(FP8X4), rhs_scale=moving_sc[:, cols], start=True, stop=True,
                 )
 
-        def products(b):
+        def projections(b):
             aer = psum1.tile([P, PACK, JB], F32, name="aer", tag="aer")
             aei = psum1.tile([P, PACK, JB], F32, name="aei", tag="aei")
             arr = psum2.tile([P, PACK, JB], F32, name="arr", tag="arr")
             ari = psum2.tile([P, PACK, JB], F32, name="ari", tag="ari")
-            project(aer, we[:, 0, :], we_sc[:, :], ve, ve_sc, b)
-            project(aei, we[:, 1, :], we_sc[4:P, :], ve, ve_sc, b)
-            project(arr, wr[:, 0, :], wr_sc[:, 0, :], vr, vr_sc, b)
-            project(ari, wr[:, 1, :], wr_sc[:, 1, :], vr, vr_sc, b)
+            project(aer, we[:, 0, :], we_sc[:, :], ve[:, b * JB : (b + 1) * JB], ve_sc, b)
+            project(aei, we[:, 1, :], we_sc[4:P, :], ve[:, b * JB : (b + 1) * JB], ve_sc, b)
+            project(arr, wr[:, 0, :], wr_sc[:, 0, :], vr[b], vr_sc, b)
+            project(ari, wr[:, 1, :], wr_sc[:, 1, :], vr[b], vr_sc, b)
             ae = ring.tile([P, 2, JB, PACK], F32, name="ae", bufs=3)
             nc.scalar.copy(out=ae[:, 0], in_=aer[:].rearrange("p t j -> p j t"))
             nc.scalar.copy(out=ae[:, 1], in_=aei[:].rearrange("p t j -> p j t"))
+            return ae, arr, ari
+
+        def products(parts):
+            ae, arr, ari = parts
             by_arr = ring.tile([P, 2, JB, PACK], F32, name="by_arr", bufs=3)
             by_ari = ring.tile([P, 2, JB, PACK], F32, name="by_ari", bufs=3)
             arr_jt = arr[:].rearrange("p t j -> p j t")
@@ -164,36 +175,41 @@ def tile_list_ckg_none_kernel(
                 start=(part == 0), stop=(part == 1),
             )
 
-        def store(b, y_sb, groups):
+        def store(queue, b, y_sb, groups):
             rows = out[:, b * JB : (b + 1) * JB].rearrange("(g p) j -> p g j", p=P)
-            nc.sync.dma_start(out=rows[:, groups, :], in_=y_sb[:, groups, :])
+            queue.dma_start(out=rows[:, groups, :], in_=y_sb[:, groups, :])
 
         def score(b, h):
             hq = ring.tile([P, 2 * JB], U32, name="hq", align_bytes=AL, bufs=3)
             hq_sc = ring.tile([P, 2 * JB], U8, name="hq_sc", align_bytes=AL, bufs=3)
             nc.vector.quantize_mx(out=hq[:].bitcast(FP8X4), scales=hq_sc[:], in_=h[:])
-            y = psum2.tile([P, N // P, JB], F32, name="y")
-            for g in range(N // P):
-                for part in range(2):
-                    score_pass(y[:, g, :], g, part, hq, hq_sc)
+            tags = {BLOCKS - 3: ["y", "y"], BLOCKS - 2: ["arr", "ari"]}.get(b, ["y"])
+            per_bank = N // P // len(tags)
             y_sb = ring.tile([P, N // P, JB], F32, name="y_sb", bufs=3)
-            nc.scalar.copy(out=y_sb[:], in_=y[:])
-            store(b, y_sb, slice(0, N // P))
+            for c, tag in enumerate(tags):
+                y = psum2.tile([P, per_bank, JB], F32, name="y", tag=tag)
+                groups = slice(c * per_bank, (c + 1) * per_bank)
+                for g in range(per_bank):
+                    for part in range(2):
+                        score_pass(y[:, g, :], groups.start + g, part, hq, hq_sc)
+                nc.scalar.copy(out=y_sb[:, groups, :], in_=y[:])
+                store(nc.sync, b, y_sb, groups)
 
-        def last_block(b, terms):
+        def last_block(b, terms, h_before):
             by_arr, by_ari = terms
-            h = ring.tile([P, 2 * JB * PACK], BF16, name="h", align_bytes=AL, bufs=3)
+            width = JB * PACK
+            hr = ring.tile([P, width], BF16, name="h", align_bytes=AL, bufs=3)
+            halves = [hr[:], h_before[:, 0:width]]
             hq = ring.tile([P, 2 * JB], U32, name="hq", align_bytes=AL, bufs=3)
             hq_sc = ring.tile([P, 2 * JB], U8, name="hq_sc", align_bytes=AL, bufs=3)
-            width = JB * PACK
             for part in range(2):
                 cols = slice(part * width, (part + 1) * width)
-                nc.vector.tensor_tensor(h[:, cols], flat(by_arr[:])[:, cols], flat(by_ari[:])[:, cols], ADD)
+                nc.vector.tensor_tensor(halves[part], flat(by_arr[:])[:, cols], flat(by_ari[:])[:, cols], ADD)
             for part in range(2):
                 nc.vector.quantize_mx(
                     out=hq[:, part * JB : (part + 1) * JB].bitcast(FP8X4),
                     scales=hq_sc[:, part * JB : (part + 1) * JB],
-                    in_=h[:, part * width : (part + 1) * width],
+                    in_=halves[part],
                 )
             banks = [
                 psum1.tile([P, JB], F32, name="y0", tag="aer"),
@@ -205,22 +221,25 @@ def tile_list_ckg_none_kernel(
                 for g in range(N // P):
                     score_pass(banks[g][:], g, part, hq, hq_sc)
             y_sb = ring.tile([P, N // P, JB], F32, name="y_sb", bufs=3)
-            for g in range(N // P):
-                if g % 2 == 0:
-                    nc.scalar.copy(out=y_sb[:, g, :], in_=banks[g][:])
-                else:
-                    nc.vector.tensor_copy(out=y_sb[:, g, :], in_=banks[g][:])
-                    store(b, y_sb, slice(g - 1, g + 1))
+            for g in (0, 1):
+                nc.vector.tensor_copy(out=y_sb[:, g, :], in_=banks[g][:])
+            store(nc.sync, b, y_sb, slice(0, 2))
+            for g in (2, 3):
+                nc.scalar.copy(out=y_sb[:, g, :], in_=banks[g][:])
+            store(nc.scalar, b, y_sb, slice(2, 4))
 
         h = {}
         after = {b: [b - 2] for b in range(2, BLOCKS - 1)}
         after[BLOCKS - 1] = [BLOCKS - 3, BLOCKS - 2]
+        parts = {0: projections(0)}
         for b in range(BLOCKS):
-            terms = products(b)
+            if b + 1 < BLOCKS:
+                parts[b + 1] = projections(b + 1)
+            terms = products(parts[b])
             if b == 0:
-                gather(vr, tab_r[:].bitcast(U32), list_r, J - PIECE, J)
+                gather_relation_words(2 * PIECE, J)
             for done in after.get(b, []):
                 score(done, h[done])
             if b < BLOCKS - 1:
                 h[b] = combine(terms)
-        last_block(BLOCKS - 1, terms)
+        last_block(BLOCKS - 1, terms, h[BLOCKS - 2])

@@ -47,7 +47,8 @@ def tile_list_ckg_none_kernel(
         we_sc = keep.tile([P, R], U8, name="we_sc", align_bytes=AL)
         wr_raw = [keep.tile([P, PACK, R], F32, name="wr_raw%d" % c, align_bytes=AL) for c in range(2)]
         wr_bf = [keep.tile([P, R * PACK], BF16, name="wr_bf%d" % c, align_bytes=AL) for c in range(2)]
-        wr = keep.tile([P, 2, R], U32, name="wr", align_bytes=AL)
+        wrr_q = keep.tile([P, R], I32, name="wrr_q", align_bytes=AL)
+        wr = [wrr_q[:], we_raw[:, 0, :]]
         wr_sc = keep.tile([P, 2, R], U8, name="wr_sc", align_bytes=AL)
         nr = keep.tile([P, N], I32, name="nr", align_bytes=AL)
         ni = keep.tile([P, N // 2], I32, name="ni", align_bytes=AL)
@@ -65,27 +66,27 @@ def tile_list_ckg_none_kernel(
 
         for plane in (tab_e_sc, tab_r_sc, we_sc_raw):
             nc.vector.memset(plane[:], 0)
-        nc.gpsimd.dma_start(out=wr_raw[0][:], in_=wrr.rearrange("(p i) r -> p i r", i=PACK))
-        nc.gpsimd.dma_start(out=tab_e[:], in_=words(tab_words))
-        nc.gpsimd.dma_start(out=wr_raw[1][:], in_=wri.rearrange("(p i) r -> p i r", i=PACK))
-        nc.gpsimd.dma_start(out=we_raw[:, 0, :], in_=words(wer_words))
-        nc.gpsimd.dma_start(out=we_raw[:, 1, :], in_=words(wei_words))
-        nc.gpsimd.dma_start(out=tab_r[:], in_=words(tab2_words))
-        nc.gpsimd.dma_start(out=nr[:], in_=words(nr_words))
-        nc.gpsimd.dma_start(out=ni[:], in_=ni_words[0].bitcast(I32))
         nc.sync.dma_start(list_e[:], offs)
-        load_scales([nc.scalar, nc.sync], tab_e_sc, tab_scales, 0)
         nc.sync.dma_start(list_r[:], offs2)
-        load_scales([nc.scalar, nc.sync], tab_r_sc, tab2_scales, 0)
+        load_scales([nc.sync], tab_e_sc, tab_scales, 0)
+        nc.sync.dma_start(out=tab_e[:], in_=words(tab_words))
+        load_scales([nc.sync], tab_r_sc, tab2_scales, 0)
+        nc.sync.dma_start(out=wr_raw[0][:], in_=wrr.rearrange("(p i) r -> p i r", i=PACK))
         load_scales([nc.sync], we_sc_raw, wer_scales, 0)
+        nc.sync.dma_start(out=wr_raw[1][:], in_=wri.rearrange("(p i) r -> p i r", i=PACK))
         load_scales([nc.sync], we_sc_raw, wei_scales, 4)
+        nc.sync.dma_start(out=we_raw[:, 0, :], in_=words(wer_words))
+        nc.sync.dma_start(out=we_raw[:, 1, :], in_=words(wei_words))
+        nc.sync.dma_start(out=tab_r[:], in_=words(tab2_words))
+        nc.sync.dma_start(out=nr[:], in_=words(nr_words))
+        nc.sync.dma_start(out=ni[:], in_=ni_words[0].bitcast(I32))
 
         def gather(dst, window, offsets, first, last):
             nc.vector.tensor_copy(dst[:, first:last], window.indirect(offsets[:, first // 16 : last // 16]))
 
         gather(ve_sc, tab_e_sc[:].bitcast(U8), list_e, 0, J)
-        gather(vr_sc, tab_r_sc[:].bitcast(U8), list_r, 0, J)
         gather(ve, tab_e[:].bitcast(U32), list_e, 0, J)
+        gather(vr_sc, tab_r_sc[:].bitcast(U8), list_r, 0, J)
 
         vr = {}
 
@@ -100,16 +101,16 @@ def tile_list_ckg_none_kernel(
                 out=wr_bf[c][:].rearrange("p (t m i) -> p m i t", t=PACK, i=PACK),
                 in_=wr_raw[c][:].rearrange("p i (m t) -> p m i t", t=PACK),
             )
-            nc.vector.quantize_mx(out=wr[:, c, :].bitcast(FP8X4), scales=wr_sc[:, c, :], in_=wr_bf[c][:])
+            nc.vector.quantize_mx(out=wr[c].bitcast(FP8X4), scales=wr_sc[:, c, :], in_=wr_bf[c][:])
 
         quantize_weight(0)
         nc.vector.tensor_copy(
-            out=we[:].rearrange("p c (t m) -> p c m t", t=PACK),
-            in_=we_raw[:].rearrange("p c (m t) -> p c m t", t=PACK),
-        )
-        nc.vector.tensor_copy(
             out=we_sc[:].rearrange("p (t m) -> p m t", t=PACK),
             in_=we_sc_raw[:].bitcast(U8).rearrange("p (m t) -> p m t", t=PACK),
+        )
+        nc.vector.tensor_copy(
+            out=we[:].rearrange("p c (t m) -> p c m t", t=PACK),
+            in_=we_raw[:].rearrange("p c (m t) -> p c m t", t=PACK),
         )
         n_sc = we_sc_raw
         load_scales([nc.sync], n_sc, ni_scales, 0)
@@ -136,8 +137,8 @@ def tile_list_ckg_none_kernel(
             ari = psum2.tile([P, PACK, JB], F32, name="ari", tag="ari")
             project(aer, we[:, 0, :], we_sc[:, :], ve[:, b * JB : (b + 1) * JB], ve_sc, b)
             project(aei, we[:, 1, :], we_sc[4:P, :], ve[:, b * JB : (b + 1) * JB], ve_sc, b)
-            project(arr, wr[:, 0, :], wr_sc[:, 0, :], vr[b], vr_sc, b)
-            project(ari, wr[:, 1, :], wr_sc[:, 1, :], vr[b], vr_sc, b)
+            project(arr, wr[0], wr_sc[:, 0, :], vr[b], vr_sc, b)
+            project(ari, wr[1], wr_sc[:, 1, :], vr[b], vr_sc, b)
             ae = ring.tile([P, 2, JB, PACK], F32, name="ae", bufs=3)
             nc.scalar.copy(out=ae[:, 0], in_=aer[:].rearrange("p t j -> p j t"))
             nc.scalar.copy(out=ae[:, 1], in_=aei[:].rearrange("p t j -> p j t"))

@@ -1,6 +1,7 @@
 from contextlib import ExitStack
 
 import concourse.mybir as mybir
+from concourse.masks import make_identity
 
 K, L, R, N, T, J = 512, 512, 512, 512, 2048, 1024
 FLOPS = 2 * J * (2 * K * R + 2 * L * R + 2 * R * N)
@@ -22,6 +23,8 @@ JB = 128
 BLOCKS = J // JB
 PIECE = 256
 AL = 64
+FRONT = 512
+TURNED = 2
 
 
 def tile_list_ckg_none_kernel(
@@ -32,8 +35,7 @@ def tile_list_ckg_none_kernel(
     with ExitStack() as ctx:
         keep = ctx.enter_context(tc.tile_pool(name="keep", bufs=1))
         ring = ctx.enter_context(tc.tile_pool(name="ring", bufs=2))
-        psum1 = ctx.enter_context(tc.psum_pool(name="psum1", bufs=1))
-        psum2 = ctx.enter_context(tc.psum_pool(name="psum2", bufs=2))
+        psum = ctx.enter_context(tc.psum_pool(name="psum", bufs=1))
 
         list_e = keep.tile([P, J // 16], U16, name="list_e")
         list_r = keep.tile([P, J // 16], U16, name="list_r")
@@ -43,43 +45,52 @@ def tile_list_ckg_none_kernel(
         tab_r_sc = keep.tile([P, T // 4], I32, name="tab_r_sc", align_bytes=AL)
         we_raw = keep.tile([P, 2, R], I32, name="we_raw", align_bytes=AL)
         we_sc_raw = keep.tile([P, R // 4], I32, name="we_sc_raw", align_bytes=AL)
-        we = keep.tile([P, 2, R], I32, name="we", align_bytes=AL)
         we_sc = keep.tile([P, R], U8, name="we_sc", align_bytes=AL)
         wr_raw = [keep.tile([P, PACK, R], F32, name="wr_raw%d" % c, align_bytes=AL) for c in range(2)]
         wr_bf = [keep.tile([P, R * PACK], BF16, name="wr_bf%d" % c, align_bytes=AL) for c in range(2)]
-        wrr_q = keep.tile([P, R], I32, name="wrr_q", align_bytes=AL)
-        wr = [wrr_q[:], we_raw[:, 0, :]]
-        wr_sc = keep.tile([P, 2, R], U8, name="wr_sc", align_bytes=AL)
+        n_sc = keep.tile([P, N // 4], I32, name="n_sc", align_bytes=AL)
         nr = keep.tile([P, N], I32, name="nr", align_bytes=AL)
         ni = keep.tile([P, N // 2], I32, name="ni", align_bytes=AL)
         ve = keep.tile([P, J], U32, name="ve", align_bytes=AL)
         ve_sc = keep.tile([P, J], U8, name="ve_sc", align_bytes=AL)
         vr_sc = keep.tile([P, J], U8, name="vr_sc", align_bytes=AL)
+        vr = keep.tile([P, J], U32, name="vr", align_bytes=AL)
+        we = keep.tile([P, 2, R], I32, name="we", align_bytes=AL)
+        ident = keep.tile([P, P], F32, name="ident", align_bytes=AL)
+
+        def bank(number, shape):
+            return psum.tile(shape, F32, name="bank%d" % number, tag="bank%d" % number)
 
         def words(ap):
             return ap[0].rearrange("p n i -> p (n i)").bitcast(I32)
 
-        def load_scales(queues, plane, scales, first):
+        def load_scales(plane, scales, first, which=range(4)):
             rows = scales[0].bitcast(I32).rearrange("(q r) c -> r q c", r=4)
-            for r in range(4):
-                queues[r * len(queues) // 4].dma_start(out=plane[first + r : P : 32, :], in_=rows[r])
+            for r in which:
+                nc.sync.dma_start(out=plane[first + r : P : 32, :], in_=rows[r])
 
-        for plane in (tab_e_sc, tab_r_sc, we_sc_raw):
+        for plane in (tab_e_sc, tab_r_sc, we_sc_raw, n_sc):
             nc.vector.memset(plane[:], 0)
+        nc.vector.memset(ident[:], 0.0)
+        make_identity(nc, ident[:], nomemset=True)
         nc.sync.dma_start(list_e[:], offs)
         nc.sync.dma_start(list_r[:], offs2)
-        load_scales([nc.sync], tab_e_sc, tab_scales, 0)
-        nc.sync.dma_start(out=tab_e[:], in_=words(tab_words))
-        load_scales([nc.sync], tab_r_sc, tab2_scales, 0)
+        nc.sync.dma_start(out=tab_e[:, 0:FRONT], in_=words(tab_words)[:, 0:FRONT])
+        load_scales(tab_e_sc, tab_scales, 0)
+        nc.sync.dma_start(out=tab_e[:, FRONT:T], in_=words(tab_words)[:, FRONT:T])
+        load_scales(tab_r_sc, tab2_scales, 12, range(0, 2))
         nc.sync.dma_start(out=wr_raw[0][:], in_=wrr.rearrange("(p i) r -> p i r", i=PACK))
-        load_scales([nc.sync], we_sc_raw, wer_scales, 0)
+        load_scales(tab_r_sc, tab2_scales, 12, range(2, 4))
+        load_scales(we_sc_raw, wer_scales, 4)
         nc.sync.dma_start(out=wr_raw[1][:], in_=wri.rearrange("(p i) r -> p i r", i=PACK))
-        load_scales([nc.sync], we_sc_raw, wei_scales, 4)
         nc.sync.dma_start(out=we_raw[:, 0, :], in_=words(wer_words))
         nc.sync.dma_start(out=we_raw[:, 1, :], in_=words(wei_words))
+        load_scales(we_sc_raw, wei_scales, 8)
         nc.sync.dma_start(out=tab_r[:], in_=words(tab2_words))
         nc.sync.dma_start(out=nr[:], in_=words(nr_words))
         nc.sync.dma_start(out=ni[:], in_=ni_words[0].bitcast(I32))
+        load_scales(n_sc, ni_scales, 0)
+        load_scales(n_sc, nr_scales, 4)
 
         def gather(dst, window, offsets, first, last):
             nc.vector.tensor_copy(dst[:, first:last], window.indirect(offsets[:, first // 16 : last // 16]))
@@ -88,75 +99,111 @@ def tile_list_ckg_none_kernel(
         gather(ve, tab_e[:].bitcast(U32), list_e, 0, J)
         gather(vr_sc, tab_r_sc[:].bitcast(U8), list_r, 0, J)
 
-        vr = {}
-
-        def gather_relation_words(first, last):
-            piece = ring.tile([P, last - first], U32, name="vr_piece", align_bytes=AL)
-            nc.vector.tensor_copy(piece[:], tab_r[:].bitcast(U32).indirect(list_r[:, first // 16 : last // 16]))
-            for b in range(first // JB, last // JB):
-                vr[b] = piece[:, b * JB - first : (b + 1) * JB - first]
-
-        def quantize_weight(c):
+        for c in range(2):
             nc.scalar.copy(
                 out=wr_bf[c][:].rearrange("p (t m i) -> p m i t", t=PACK, i=PACK),
                 in_=wr_raw[c][:].rearrange("p i (m t) -> p m i t", t=PACK),
             )
+        for c in range(2):
+            nc.vector.tensor_copy(
+                out=we[:, c, :].rearrange("p (t m) -> p t m", t=PACK),
+                in_=we_raw[:, c, :].rearrange("p (m t) -> p t m", t=PACK),
+            )
+        nc.vector.tensor_copy(
+            out=we_sc[:].rearrange("p (t m) -> p t m", t=PACK),
+            in_=we_sc_raw[:].bitcast(U8).rearrange("p (m t) -> p t m", t=PACK),
+        )
+        wr_sc = keep.tile([P, 2, R], U8, name="wr_sc", tag="we_sc_raw", align_bytes=AL)
+        wr = [we_raw[:, 0, :], we_raw[:, 1, :]]
+        for c in range(2):
             nc.vector.quantize_mx(out=wr[c].bitcast(FP8X4), scales=wr_sc[:, c, :], in_=wr_bf[c][:])
-
-        quantize_weight(0)
-        nc.vector.tensor_copy(
-            out=we_sc[:].rearrange("p (t m) -> p m t", t=PACK),
-            in_=we_sc_raw[:].bitcast(U8).rearrange("p (m t) -> p m t", t=PACK),
-        )
-        nc.vector.tensor_copy(
-            out=we[:].rearrange("p c (t m) -> p c m t", t=PACK),
-            in_=we_raw[:].rearrange("p c (m t) -> p c m t", t=PACK),
-        )
-        n_sc = we_sc_raw
-        load_scales([nc.sync], n_sc, ni_scales, 0)
-        load_scales([nc.sync], n_sc, nr_scales, 4)
-        quantize_weight(1)
-        gather_relation_words(0, PIECE)
-        gather_relation_words(PIECE, 2 * PIECE)
+        gather(vr, tab_r[:].bitcast(U32), list_r, 0, PIECE)
+        gather(vr, tab_r[:].bitcast(U32), list_r, PIECE, J)
         n_sc8 = n_sc[:].bitcast(U8)
         ni8 = ni[:].bitcast(U8)
 
-        def project(bank, codes, plane, moving, moving_sc, b):
+        weights = [
+            (we[:, 0, :], we_sc[4:P, :]), (we[:, 1, :], we_sc[8:P, :]), (wr[0], wr_sc[:, 0, :]), (wr[1], wr_sc[:, 1, :]),
+        ]
+        picked = [(ve, ve_sc[:, :]), (ve, ve_sc[:, :]), (vr, vr_sc[12:P, :]), (vr, vr_sc[12:P, :])]
+
+        def project(number, which, b):
+            codes, plane = weights[which]
+            columns, columns_sc = picked[which]
             cols = slice(b * JB, (b + 1) * JB)
+            if b < TURNED:
+                acc = bank(number, [P, R])
+                nc.tensor.matmul_mx(
+                    out=acc[:], lhsT=columns[:, cols].bitcast(FP8X4), lhsT_scale=columns_sc[:, cols],
+                    rhs=codes.bitcast(FP8X4), rhs_scale=plane, start=True, stop=True,
+                )
+                return acc[:]
+            acc = bank(number, [P, PACK, JB])
             for t in range(PACK):
                 m = slice(t * P, (t + 1) * P)
                 nc.tensor.matmul_mx(
-                    out=bank[:, t, :], lhsT=codes[:, m].bitcast(FP8X4), lhsT_scale=plane[:, m],
-                    rhs=moving.bitcast(FP8X4), rhs_scale=moving_sc[:, cols], start=True, stop=True,
+                    out=acc[:, t, :], lhsT=codes[:, m].bitcast(FP8X4), lhsT_scale=plane[:, m],
+                    rhs=columns[:, cols].bitcast(FP8X4), rhs_scale=columns_sc[:, cols], start=True, stop=True,
                 )
+            return acc[:].rearrange("p t j -> p j t")
 
-        def projections(b):
-            aer = psum1.tile([P, PACK, JB], F32, name="aer", tag="aer")
-            aei = psum1.tile([P, PACK, JB], F32, name="aei", tag="aei")
-            arr = psum2.tile([P, PACK, JB], F32, name="arr", tag="arr")
-            ari = psum2.tile([P, PACK, JB], F32, name="ari", tag="ari")
-            project(aer, we[:, 0, :], we_sc[:, :], ve[:, b * JB : (b + 1) * JB], ve_sc, b)
-            project(aei, we[:, 1, :], we_sc[4:P, :], ve[:, b * JB : (b + 1) * JB], ve_sc, b)
-            project(arr, wr[0], wr_sc[:, 0, :], vr[b], vr_sc, b)
-            project(ari, wr[1], wr_sc[:, 1, :], vr[b], vr_sc, b)
-            ae = ring.tile([P, 2, JB, PACK], F32, name="ae", bufs=3)
-            nc.scalar.copy(out=ae[:, 0], in_=aer[:].rearrange("p t j -> p j t"))
-            nc.scalar.copy(out=ae[:, 1], in_=aei[:].rearrange("p t j -> p j t"))
-            return ae, arr, ari
+        def shaped(tile, b):
+            if b < TURNED:
+                return tile
+            return tile.rearrange("p (j t) -> p j t", t=PACK)
 
-        def products(parts):
-            ae, arr, ari = parts
-            by_arr = ring.tile([P, 2, JB, PACK], F32, name="by_arr", bufs=3)
-            by_ari = ring.tile([P, 2, JB, PACK], F32, name="by_ari", bufs=3)
-            arr_jt = arr[:].rearrange("p t j -> p j t")
-            ari_jt = ari[:].rearrange("p t j -> p j t")
-            nc.vector.tensor_tensor(by_arr[:], arr_jt.unsqueeze(1).to_broadcast([P, 2, JB, PACK]), ae[:], MULT)
-            nc.vector.scalar_tensor_tensor(by_ari[:, 0], ari_jt, -1.0, ae[:, 1], MULT, MULT)
-            nc.vector.tensor_tensor(by_ari[:, 1], ari_jt, ae[:, 0], MULT)
+        def leave(dst, acc, b):
+            nc.scalar.copy(out=shaped(dst, b), in_=acc)
+
+        def entity(b):
+            first = {0: 2, 1: 6, 2: 0, 5: 0}.get(b, 2)
+            ae = ring.tile([P, 2, R], F32, name="ae", bufs=3)
+            for c in range(2):
+                leave(ae[:, c, :], project(first + c, c, b), b)
+            return ae
+
+        def relation(b):
+            if b < TURNED:
+                arr = ring.tile([P, R], F32, name="arr_sb")
+                leave(arr[:], project(b, 2, b), b)
+                return arr[:], project(4 + b, 3, b)
+            first = 4 if b % 2 else 6
+            return project(first, 2, b), project(first + 1, 3, b)
+
+        def products(ae, parts, b):
+            arr, ari = parts
+            by_arr = ring.tile([P, 2, R], F32, name="by_arr", bufs=4)
+            by_ari = ring.tile([P, 2, R], F32, name="by_ari", bufs=4)
+            if b < TURNED:
+                nc.gpsimd.tensor_tensor(by_arr[:], arr.unsqueeze(1).to_broadcast([P, 2, R]), ae[:], MULT)
+            else:
+                both = "p c (j t) -> p c j t"
+                nc.vector.tensor_tensor(
+                    by_arr[:].rearrange(both, t=PACK), arr.unsqueeze(1).to_broadcast([P, 2, JB, PACK]),
+                    ae[:].rearrange(both, t=PACK), MULT,
+                )
+            nc.vector.scalar_tensor_tensor(shaped(by_ari[:, 0, :], b), ari, -1.0, shaped(ae[:, 1, :], b), MULT, MULT)
+            nc.vector.tensor_tensor(shaped(by_ari[:, 1, :], b), ari, shaped(ae[:, 0, :], b), MULT)
             return by_arr, by_ari
 
+        def combine_turned(terms, first):
+            h = ring.tile([P, 2 * JB * PACK], BF16, name="h", align_bytes=AL, bufs=3)
+            for c in range(2):
+                acc = bank(first + c, [P, PACK, JB])
+                for n, term in enumerate(terms):
+                    for t in range(PACK):
+                        nc.tensor.matmul(
+                            out=acc[:, t, :], lhsT=term[:, c, t * P : (t + 1) * P], rhs=ident[:], is_transpose=True,
+                            start=(n == 0 and t == 0), stop=(n == 1 and t == PACK - 1),
+                        )
+                nc.scalar.copy(
+                    out=h[:, c * R : (c + 1) * R].rearrange("p (j t) -> p j t", t=PACK),
+                    in_=acc[:].rearrange("p t j -> p j t"),
+                )
+            return h
+
         def flat(terms):
-            return terms.rearrange("p c j t -> p (c j t)")
+            return terms.rearrange("p c x -> p (c x)")
 
         def combine(terms):
             by_arr, by_ari = terms
@@ -184,11 +231,11 @@ def tile_list_ckg_none_kernel(
             hq = ring.tile([P, 2 * JB], U32, name="hq", align_bytes=AL, bufs=3)
             hq_sc = ring.tile([P, 2 * JB], U8, name="hq_sc", align_bytes=AL, bufs=3)
             nc.vector.quantize_mx(out=hq[:].bitcast(FP8X4), scales=hq_sc[:], in_=h[:])
-            tags = {BLOCKS - 3: ["y", "y"], BLOCKS - 2: ["arr", "ari"]}.get(b, ["y"])
+            tags = {BLOCKS - 3: [0, 1], BLOCKS - 2: [6, 7]}.get(b, [b % 2])
             per_bank = N // P // len(tags)
             y_sb = ring.tile([P, N // P, JB], F32, name="y_sb", bufs=3)
             for c, tag in enumerate(tags):
-                y = psum2.tile([P, per_bank, JB], F32, name="y", tag=tag)
+                y = bank(tag, [P, per_bank, JB])
                 groups = slice(c * per_bank, (c + 1) * per_bank)
                 for g in range(per_bank):
                     for part in range(2):
@@ -212,12 +259,7 @@ def tile_list_ckg_none_kernel(
                     scales=hq_sc[:, part * JB : (part + 1) * JB],
                     in_=halves[part],
                 )
-            banks = [
-                psum1.tile([P, JB], F32, name="y0", tag="aer"),
-                psum1.tile([P, JB], F32, name="y1", tag="aei"),
-                psum2.tile([P, JB], F32, name="y2", tag="arr"),
-                psum2.tile([P, JB], F32, name="y3", tag="ari"),
-            ]
+            banks = [bank(number, [P, JB]) for number in (2, 3, 4, 5)]
             for part in range(2):
                 for g in range(N // P):
                     score_pass(banks[g][:], g, part, hq, hq_sc)
@@ -230,17 +272,24 @@ def tile_list_ckg_none_kernel(
             store(nc.scalar, b, y_sb, slice(2, 4))
 
         h = {}
-        after = {b: [b - 2] for b in range(2, BLOCKS - 1)}
-        after[BLOCKS - 1] = [BLOCKS - 3, BLOCKS - 2]
-        parts = {0: projections(0)}
-        for b in range(BLOCKS):
-            if b + 1 < BLOCKS:
-                parts[b + 1] = projections(b + 1)
-            terms = products(parts[b])
-            if b == 0:
-                gather_relation_words(2 * PIECE, J)
+        after = {3: [0], 4: [1, 2], 5: [3], 6: [4], 7: [5, 6]}
+        ae = {b: entity(b) for b in range(2)}
+        ar = {b: relation(b) for b in range(2)}
+        ae[2] = entity(2)
+        ar[2] = relation(2)
+        ae[3] = entity(3)
+        terms = {b: products(ae[b], ar[b], b) for b in range(2)}
+        ar[3] = relation(3)
+        h[0] = combine_turned(terms[0], 0)
+        for b in range(TURNED, BLOCKS):
+            terms[b] = products(ae[b], ar[b], b)
+            if b + 2 < BLOCKS:
+                ae[b + 2] = entity(b + 2)
+                ar[b + 2] = relation(b + 2)
             for done in after.get(b, []):
                 score(done, h[done])
             if b < BLOCKS - 1:
-                h[b] = combine(terms)
-        last_block(BLOCKS - 1, terms, h[BLOCKS - 2])
+                h[b] = combine(terms[b])
+            if b == TURNED:
+                h[1] = combine_turned(terms[1], 2)
+        last_block(BLOCKS - 1, terms[BLOCKS - 1], h[BLOCKS - 2])

@@ -23,8 +23,9 @@ JB = 128
 BLOCKS = J // JB
 PIECE = 256
 AL = 64
-FRONT = 512
-TURNED = 2
+FRONT = 768
+SHARED = 2
+TURNED = (0, 1, 6)
 
 
 def tile_list_ckg_none_kernel(
@@ -64,33 +65,32 @@ def tile_list_ckg_none_kernel(
         def words(ap):
             return ap[0].rearrange("p n i -> p (n i)").bitcast(I32)
 
-        def load_scales(plane, scales, first, which=range(4)):
+        def load_scales(queue, plane, scales, first):
             rows = scales[0].bitcast(I32).rearrange("(q r) c -> r q c", r=4)
-            for r in which:
-                nc.sync.dma_start(out=plane[first + r : P : 32, :], in_=rows[r])
+            for r in range(4):
+                queue.dma_start(out=plane[first + r : P : 32, :], in_=rows[r])
 
-        for plane in (tab_e_sc, tab_r_sc, we_sc_raw, n_sc):
+        for plane in (tab_e_sc, we_sc_raw, tab_r_sc, n_sc):
             nc.vector.memset(plane[:], 0)
         nc.vector.memset(ident[:], 0.0)
+        load_scales(nc.gpsimd, we_sc_raw, wei_scales, 8)
         make_identity(nc, ident[:], nomemset=True)
         nc.sync.dma_start(list_e[:], offs)
         nc.sync.dma_start(list_r[:], offs2)
         nc.sync.dma_start(out=tab_e[:, 0:FRONT], in_=words(tab_words)[:, 0:FRONT])
-        load_scales(tab_e_sc, tab_scales, 0)
+        load_scales(nc.sync, tab_e_sc, tab_scales, 0)
         nc.sync.dma_start(out=tab_e[:, FRONT:T], in_=words(tab_words)[:, FRONT:T])
-        load_scales(tab_r_sc, tab2_scales, 12, range(0, 2))
         nc.sync.dma_start(out=wr_raw[0][:], in_=wrr.rearrange("(p i) r -> p i r", i=PACK))
-        load_scales(tab_r_sc, tab2_scales, 12, range(2, 4))
-        load_scales(we_sc_raw, wer_scales, 4)
+        load_scales(nc.sync, tab_r_sc, tab2_scales, 12)
         nc.sync.dma_start(out=wr_raw[1][:], in_=wri.rearrange("(p i) r -> p i r", i=PACK))
         nc.sync.dma_start(out=we_raw[:, 0, :], in_=words(wer_words))
         nc.sync.dma_start(out=we_raw[:, 1, :], in_=words(wei_words))
-        load_scales(we_sc_raw, wei_scales, 8)
+        load_scales(nc.sync, we_sc_raw, wer_scales, 4)
         nc.sync.dma_start(out=tab_r[:], in_=words(tab2_words))
         nc.sync.dma_start(out=nr[:], in_=words(nr_words))
         nc.sync.dma_start(out=ni[:], in_=ni_words[0].bitcast(I32))
-        load_scales(n_sc, ni_scales, 0)
-        load_scales(n_sc, nr_scales, 4)
+        load_scales(nc.sync, n_sc, ni_scales, 0)
+        load_scales(nc.sync, n_sc, nr_scales, 4)
 
         def gather(dst, window, offsets, first, last):
             nc.vector.tensor_copy(dst[:, first:last], window.indirect(offsets[:, first // 16 : last // 16]))
@@ -106,8 +106,8 @@ def tile_list_ckg_none_kernel(
             )
         for c in range(2):
             nc.vector.tensor_copy(
-                out=we[:, c, :].rearrange("p (t m) -> p t m", t=PACK),
-                in_=we_raw[:, c, :].rearrange("p (m t) -> p t m", t=PACK),
+                out=we[:, c, :].rearrange("p (t m) -> p m t", t=PACK),
+                in_=we_raw[:, c, :].rearrange("p (m t) -> p m t", t=PACK),
             )
         nc.vector.tensor_copy(
             out=we_sc[:].rearrange("p (t m) -> p t m", t=PACK),
@@ -131,7 +131,7 @@ def tile_list_ckg_none_kernel(
             codes, plane = weights[which]
             columns, columns_sc = picked[which]
             cols = slice(b * JB, (b + 1) * JB)
-            if b < TURNED:
+            if b in TURNED:
                 acc = bank(number, [P, R])
                 nc.tensor.matmul_mx(
                     out=acc[:], lhsT=columns[:, cols].bitcast(FP8X4), lhsT_scale=columns_sc[:, cols],
@@ -148,7 +148,7 @@ def tile_list_ckg_none_kernel(
             return acc[:].rearrange("p t j -> p j t")
 
         def shaped(tile, b):
-            if b < TURNED:
+            if b in TURNED:
                 return tile
             return tile.rearrange("p (j t) -> p j t", t=PACK)
 
@@ -156,41 +156,57 @@ def tile_list_ckg_none_kernel(
             nc.scalar.copy(out=shaped(dst, b), in_=acc)
 
         def entity(b):
-            first = {0: 2, 1: 6, 2: 0, 5: 0}.get(b, 2)
-            ae = ring.tile([P, 2, R], F32, name="ae", bufs=3)
+            first = {0: 2, 1: 6}.get(b, 0)
+            ae = ring.tile([P, 2, R], F32, name="ae", bufs=4)
             for c in range(2):
                 leave(ae[:, c, :], project(first + c, c, b), b)
             return ae
 
         def relation(b):
-            if b < TURNED:
-                arr = ring.tile([P, R], F32, name="arr_sb")
-                leave(arr[:], project(b, 2, b), b)
-                return arr[:], project(4 + b, 3, b)
-            first = 4 if b % 2 else 6
-            return project(first, 2, b), project(first + 1, 3, b)
+            first = 2 if b % 2 else 6
+            banks = (b, 4 + b) if b < 2 else (first, first + 1)
+            arr = project(banks[0], 2, b)
+            if b < SHARED:
+                arr_sb = ring.tile([P, R], F32, name="arr_sb", bufs=SHARED)
+                leave(arr_sb[:], arr, b)
+                arr = arr_sb[:]
+            return arr, project(banks[1], 3, b)
 
-        def products(ae, parts, b):
-            arr, ari = parts
+        def products(b):
+            arr, ari = ar[b]
             by_arr = ring.tile([P, 2, R], F32, name="by_arr", bufs=4)
             by_ari = ring.tile([P, 2, R], F32, name="by_ari", bufs=4)
-            if b < TURNED:
-                nc.gpsimd.tensor_tensor(by_arr[:], arr.unsqueeze(1).to_broadcast([P, 2, R]), ae[:], MULT)
-            else:
-                both = "p c (j t) -> p c j t"
-                nc.vector.tensor_tensor(
-                    by_arr[:].rearrange(both, t=PACK), arr.unsqueeze(1).to_broadcast([P, 2, JB, PACK]),
-                    ae[:].rearrange(both, t=PACK), MULT,
-                )
-            nc.vector.scalar_tensor_tensor(shaped(by_ari[:, 0, :], b), ari, -1.0, shaped(ae[:, 1, :], b), MULT, MULT)
-            nc.vector.tensor_tensor(shaped(by_ari[:, 1, :], b), ari, shaped(ae[:, 0, :], b), MULT)
-            return by_arr, by_ari
+            terms[b] = (by_arr, by_ari)
+            both = "p c (j t) -> p c j t"
 
-        def combine_turned(terms, first):
-            h = ring.tile([P, 2 * JB * PACK], BF16, name="h", align_bytes=AL, bufs=3)
+            def with_arr():
+                if b in TURNED:
+                    engine = nc.gpsimd if b < SHARED else nc.vector
+                    engine.tensor_tensor(by_arr[:], arr.unsqueeze(1).to_broadcast([P, 2, R]), ae[b][:], MULT)
+                else:
+                    nc.vector.tensor_tensor(
+                        by_arr[:].rearrange(both, t=PACK), arr.unsqueeze(1).to_broadcast([P, 2, JB, PACK]),
+                        ae[b][:].rearrange(both, t=PACK), MULT,
+                    )
+
+            def ari_aei():
+                nc.vector.scalar_tensor_tensor(
+                    shaped(by_ari[:, 0, :], b), ari, -1.0, shaped(ae[b][:, 1, :], b), MULT, MULT
+                )
+
+            def ari_aer():
+                nc.vector.tensor_tensor(shaped(by_ari[:, 1, :], b), ari, shaped(ae[b][:, 0, :], b), MULT)
+
+            return with_arr, ari_aei, ari_aer
+
+        def new_h(b):
+            return keep.tile([P, 2 * JB * PACK], BF16, name="h%d" % b, tag="h%d" % {5: 0, 6: 2, 7: 0}.get(b, b % 3), align_bytes=AL)
+
+        def combine_turned(b, first):
+            h = new_h(b)
             for c in range(2):
                 acc = bank(first + c, [P, PACK, JB])
-                for n, term in enumerate(terms):
+                for n, term in enumerate(terms[b]):
                     for t in range(PACK):
                         nc.tensor.matmul(
                             out=acc[:, t, :], lhsT=term[:, c, t * P : (t + 1) * P], rhs=ident[:], is_transpose=True,
@@ -205,9 +221,9 @@ def tile_list_ckg_none_kernel(
         def flat(terms):
             return terms.rearrange("p c x -> p (c x)")
 
-        def combine(terms):
-            by_arr, by_ari = terms
-            h = ring.tile([P, 2 * JB * PACK], BF16, name="h", align_bytes=AL, bufs=3)
+        def combine(b):
+            by_arr, by_ari = terms[b]
+            h = new_h(b)
             nc.gpsimd.tensor_tensor(h[:], flat(by_arr[:]), flat(by_ari[:]), ADD)
             return h
 
@@ -231,9 +247,9 @@ def tile_list_ckg_none_kernel(
             hq = ring.tile([P, 2 * JB], U32, name="hq", align_bytes=AL, bufs=3)
             hq_sc = ring.tile([P, 2 * JB], U8, name="hq_sc", align_bytes=AL, bufs=3)
             nc.vector.quantize_mx(out=hq[:].bitcast(FP8X4), scales=hq_sc[:], in_=h[:])
-            tags = {BLOCKS - 3: [0, 1], BLOCKS - 2: [6, 7]}.get(b, [b % 2])
+            tags = {BLOCKS - 3: [5, 4], BLOCKS - 2: [6, 7]}.get(b, [4 + b % 2])
             per_bank = N // P // len(tags)
-            y_sb = ring.tile([P, N // P, JB], F32, name="y_sb", bufs=3)
+            y_sb = ring.tile([P, N // P, JB], F32, name="y_sb", bufs=4)
             for c, tag in enumerate(tags):
                 y = bank(tag, [P, per_bank, JB])
                 groups = slice(c * per_bank, (c + 1) * per_bank)
@@ -243,27 +259,34 @@ def tile_list_ckg_none_kernel(
                 nc.scalar.copy(out=y_sb[:, groups, :], in_=y[:])
                 store(nc.sync, b, y_sb, groups)
 
-        def last_block(b, terms, h_before):
-            by_arr, by_ari = terms
-            width = JB * PACK
-            hr = ring.tile([P, width], BF16, name="h", align_bytes=AL, bufs=3)
-            halves = [hr[:], h_before[:, 0:width]]
+        def last_block(b):
+            arr, ari = ar[b]
+            aer, aei = shaped(ae[b][:, 0, :], b), shaped(ae[b][:, 1, :], b)
+            by_arr = ring.tile([P, 2, R], F32, name="by_arr", bufs=4)
+            by_ari = ring.tile([P, 2, R], F32, name="by_ari", bufs=4)
+            nc.vector.tensor_tensor(shaped(by_arr[:, 0, :], b), arr, aer, MULT)
+            nc.vector.scalar_tensor_tensor(shaped(by_ari[:, 0, :], b), ari, -1.0, aei, MULT, MULT)
+            score(b - 3, h[b - 3])
+            score(b - 2, h[b - 2])
+            halves = [new_h(b)[:, 0:R], h[b - 1][:, 0:R]]
+            nc.gpsimd.tensor_tensor(halves[0], by_arr[:, 0, :], by_ari[:, 0, :], ADD)
+            nc.vector.tensor_tensor(shaped(by_arr[:, 1, :], b), arr, aei, MULT)
+            nc.vector.tensor_tensor(shaped(by_ari[:, 1, :], b), ari, aer, MULT)
+            score(b - 1, h[b - 1])
+            nc.vector.tensor_tensor(halves[1], by_arr[:, 1, :], by_ari[:, 1, :], ADD)
             hq = ring.tile([P, 2 * JB], U32, name="hq", align_bytes=AL, bufs=3)
             hq_sc = ring.tile([P, 2 * JB], U8, name="hq_sc", align_bytes=AL, bufs=3)
-            for part in range(2):
-                cols = slice(part * width, (part + 1) * width)
-                nc.vector.tensor_tensor(halves[part], flat(by_arr[:])[:, cols], flat(by_ari[:])[:, cols], ADD)
             for part in range(2):
                 nc.vector.quantize_mx(
                     out=hq[:, part * JB : (part + 1) * JB].bitcast(FP8X4),
                     scales=hq_sc[:, part * JB : (part + 1) * JB],
                     in_=halves[part],
                 )
-            banks = [bank(number, [P, JB]) for number in (2, 3, 4, 5)]
+            banks = [bank(number, [P, JB]) for number in (0, 1, 2, 3)]
             for part in range(2):
                 for g in range(N // P):
                     score_pass(banks[g][:], g, part, hq, hq_sc)
-            y_sb = ring.tile([P, N // P, JB], F32, name="y_sb", bufs=3)
+            y_sb = ring.tile([P, N // P, JB], F32, name="y_sb", bufs=4)
             for g in (0, 1):
                 nc.vector.tensor_copy(out=y_sb[:, g, :], in_=banks[g][:])
             store(nc.sync, b, y_sb, slice(0, 2))
@@ -271,25 +294,31 @@ def tile_list_ckg_none_kernel(
                 nc.scalar.copy(out=y_sb[:, g, :], in_=banks[g][:])
             store(nc.scalar, b, y_sb, slice(2, 4))
 
-        h = {}
-        after = {3: [0], 4: [1, 2], 5: [3], 6: [4], 7: [5, 6]}
+        h, terms = {}, {}
+        after = {4: [0], 5: [2, 1], 6: [3]}
         ae = {b: entity(b) for b in range(2)}
         ar = {b: relation(b) for b in range(2)}
         ae[2] = entity(2)
         ar[2] = relation(2)
         ae[3] = entity(3)
-        terms = {b: products(ae[b], ar[b], b) for b in range(2)}
         ar[3] = relation(3)
-        h[0] = combine_turned(terms[0], 0)
-        for b in range(TURNED, BLOCKS):
-            terms[b] = products(ae[b], ar[b], b)
+        for b in range(SHARED):
+            for step in products(b):
+                step()
+        h[0] = combine_turned(0, 4)
+        for b in range(SHARED, BLOCKS - 1):
+            steps = products(b)
+            steps[0]()
+            for done in after.get(b, []):
+                score(done, h[done])
+            if b > SHARED:
+                h[b - 1] = combine(b - 1)
+            steps[1]()
+            steps[2]()
             if b + 2 < BLOCKS:
                 ae[b + 2] = entity(b + 2)
                 ar[b + 2] = relation(b + 2)
-            for done in after.get(b, []):
-                score(done, h[done])
-            if b < BLOCKS - 1:
-                h[b] = combine(terms[b])
-            if b == TURNED:
-                h[1] = combine_turned(terms[1], 2)
-        last_block(BLOCKS - 1, terms[BLOCKS - 1], h[BLOCKS - 2])
+            if b == SHARED:
+                h[1] = combine_turned(1, 4)
+        h[BLOCKS - 2] = combine_turned(BLOCKS - 2, 0)
+        last_block(BLOCKS - 1)

@@ -21,11 +21,20 @@ P = 128
 PACK = 4
 JB = 128
 BLOCKS = J // JB
-PIECE = 256
+LAST = BLOCKS - 1
+GROUPS = N // P
 AL = 64
 FRONT = 768
 SHARED = 2
-TURNED = (0, 1, 6)
+PIECE = SHARED * JB
+TURNED = (0, 1, LAST - 1)
+
+ROW_WER, ROW_WEI, ROW_V2, ROW_NR = 4, 8, 12, 4
+
+ENTITY, ODD, SUMS, EVEN = 0, 2, 4, 6
+
+QUANTISED_IN = {4: (0,), 5: (2, 1), 6: (3,)}
+H_BUFFER = (0, 1, 2, 0, 1, 0, 2, 0)
 
 
 def tile_list_ckg_none_kernel(
@@ -35,7 +44,7 @@ def tile_list_ckg_none_kernel(
     nc = tc.nc
     with ExitStack() as ctx:
         keep = ctx.enter_context(tc.tile_pool(name="keep", bufs=1))
-        ring = ctx.enter_context(tc.tile_pool(name="ring", bufs=2))
+        ring = ctx.enter_context(tc.tile_pool(name="ring", bufs=SHARED))
         psum = ctx.enter_context(tc.psum_pool(name="psum", bufs=1))
 
         list_e = keep.tile([P, J // 16], U16, name="list_e")
@@ -66,14 +75,14 @@ def tile_list_ckg_none_kernel(
             return ap[0].rearrange("p n i -> p (n i)").bitcast(I32)
 
         def load_scales(queue, plane, scales, first):
-            rows = scales[0].bitcast(I32).rearrange("(q r) c -> r q c", r=4)
-            for r in range(4):
-                queue.dma_start(out=plane[first + r : P : 32, :], in_=rows[r])
+            rows = scales[0].bitcast(I32).rearrange("(q s) c -> s q c", s=4)
+            for s in range(4):
+                queue.dma_start(out=plane[first + s : P : 32, :], in_=rows[s])
 
         for plane in (tab_e_sc, we_sc_raw, tab_r_sc, n_sc):
             nc.vector.memset(plane[:], 0)
         nc.vector.memset(ident[:], 0.0)
-        load_scales(nc.gpsimd, we_sc_raw, wei_scales, 8)
+        load_scales(nc.gpsimd, we_sc_raw, wei_scales, ROW_WEI)
         make_identity(nc, ident[:], nomemset=True)
         nc.sync.dma_start(list_e[:], offs)
         nc.sync.dma_start(list_r[:], offs2)
@@ -81,16 +90,16 @@ def tile_list_ckg_none_kernel(
         load_scales(nc.sync, tab_e_sc, tab_scales, 0)
         nc.sync.dma_start(out=tab_e[:, FRONT:T], in_=words(tab_words)[:, FRONT:T])
         nc.sync.dma_start(out=wr_raw[0][:], in_=wrr.rearrange("(p i) r -> p i r", i=PACK))
-        load_scales(nc.sync, tab_r_sc, tab2_scales, 12)
+        load_scales(nc.sync, tab_r_sc, tab2_scales, ROW_V2)
         nc.sync.dma_start(out=wr_raw[1][:], in_=wri.rearrange("(p i) r -> p i r", i=PACK))
         nc.sync.dma_start(out=we_raw[:, 0, :], in_=words(wer_words))
         nc.sync.dma_start(out=we_raw[:, 1, :], in_=words(wei_words))
-        load_scales(nc.sync, we_sc_raw, wer_scales, 4)
+        load_scales(nc.sync, we_sc_raw, wer_scales, ROW_WER)
         nc.sync.dma_start(out=tab_r[:], in_=words(tab2_words))
         nc.sync.dma_start(out=nr[:], in_=words(nr_words))
         nc.sync.dma_start(out=ni[:], in_=ni_words[0].bitcast(I32))
         load_scales(nc.sync, n_sc, ni_scales, 0)
-        load_scales(nc.sync, n_sc, nr_scales, 4)
+        load_scales(nc.sync, n_sc, nr_scales, ROW_NR)
 
         def gather(dst, window, offsets, first, last):
             nc.vector.tensor_copy(dst[:, first:last], window.indirect(offsets[:, first // 16 : last // 16]))
@@ -123,9 +132,12 @@ def tile_list_ckg_none_kernel(
         ni8 = ni[:].bitcast(U8)
 
         weights = [
-            (we[:, 0, :], we_sc[4:P, :]), (we[:, 1, :], we_sc[8:P, :]), (wr[0], wr_sc[:, 0, :]), (wr[1], wr_sc[:, 1, :]),
+            (we[:, 0, :], we_sc[ROW_WER:P, :]),
+            (we[:, 1, :], we_sc[ROW_WEI:P, :]),
+            (wr[0], wr_sc[:, 0, :]),
+            (wr[1], wr_sc[:, 1, :]),
         ]
-        picked = [(ve, ve_sc[:, :]), (ve, ve_sc[:, :]), (vr, vr_sc[12:P, :]), (vr, vr_sc[12:P, :])]
+        picked = [(ve, ve_sc[:, :]), (ve, ve_sc[:, :]), (vr, vr_sc[ROW_V2:P, :]), (vr, vr_sc[ROW_V2:P, :])]
 
         def project(number, which, b):
             codes, plane = weights[which]
@@ -147,91 +159,96 @@ def tile_list_ckg_none_kernel(
                 )
             return acc[:].rearrange("p t j -> p j t")
 
-        def shaped(tile, b):
+        def shaped(row, b):
             if b in TURNED:
-                return tile
-            return tile.rearrange("p (j t) -> p j t", t=PACK)
-
-        def leave(dst, acc, b):
-            nc.scalar.copy(out=shaped(dst, b), in_=acc)
+                return row
+            return row.rearrange("p (j t) -> p j t", t=PACK)
 
         def entity(b):
-            first = {0: 2, 1: 6}.get(b, 0)
-            ae = ring.tile([P, 2, R], F32, name="ae", bufs=4)
+            first = {0: ODD, 1: EVEN}.get(b, ENTITY)
+            both = ring.tile([P, 2, R], F32, name="ae", bufs=4)
             for c in range(2):
-                leave(ae[:, c, :], project(first + c, c, b), b)
-            return ae
+                nc.scalar.copy(out=shaped(both[:, c, :], b), in_=project(first + c, c, b))
+            return both
 
         def relation(b):
-            first = 2 if b % 2 else 6
-            banks = (b, 4 + b) if b < 2 else (first, first + 1)
+            first = ODD if b % 2 else EVEN
+            banks = (ENTITY + b, SUMS + b) if b < SHARED else (first, first + 1)
             arr = project(banks[0], 2, b)
             if b < SHARED:
-                arr_sb = ring.tile([P, R], F32, name="arr_sb", bufs=SHARED)
-                leave(arr_sb[:], arr, b)
+                arr_sb = ring.tile([P, R], F32, name="arr_sb")
+                nc.scalar.copy(out=arr_sb[:], in_=arr)
                 arr = arr_sb[:]
             return arr, project(banks[1], 3, b)
 
-        def products(b):
-            arr, ari = ar[b]
+        def new_terms():
             by_arr = ring.tile([P, 2, R], F32, name="by_arr", bufs=4)
             by_ari = ring.tile([P, 2, R], F32, name="by_ari", bufs=4)
-            terms[b] = (by_arr, by_ari)
-            both = "p c (j t) -> p c j t"
+            return by_arr, by_ari
 
-            def with_arr():
-                if b in TURNED:
-                    engine = nc.gpsimd if b < SHARED else nc.vector
-                    engine.tensor_tensor(by_arr[:], arr.unsqueeze(1).to_broadcast([P, 2, R]), ae[b][:], MULT)
-                else:
-                    nc.vector.tensor_tensor(
-                        by_arr[:].rearrange(both, t=PACK), arr.unsqueeze(1).to_broadcast([P, 2, JB, PACK]),
-                        ae[b][:].rearrange(both, t=PACK), MULT,
-                    )
-
-            def ari_aei():
-                nc.vector.scalar_tensor_tensor(
-                    shaped(by_ari[:, 0, :], b), ari, -1.0, shaped(ae[b][:, 1, :], b), MULT, MULT
+        def products_with_arr(b):
+            arr = ar[b][0]
+            terms[b] = new_terms()
+            by_arr = terms[b][0]
+            if b in TURNED:
+                engine = nc.gpsimd if b < SHARED else nc.vector
+                engine.tensor_tensor(by_arr[:], arr.unsqueeze(1).to_broadcast([P, 2, R]), ae[b][:], MULT)
+            else:
+                split = "p c (j t) -> p c j t"
+                nc.vector.tensor_tensor(
+                    by_arr[:].rearrange(split, t=PACK), arr.unsqueeze(1).to_broadcast([P, 2, JB, PACK]),
+                    ae[b][:].rearrange(split, t=PACK), MULT,
                 )
 
-            def ari_aer():
-                nc.vector.tensor_tensor(shaped(by_ari[:, 1, :], b), ari, shaped(ae[b][:, 0, :], b), MULT)
-
-            return with_arr, ari_aei, ari_aer
+        def products_with_ari(b):
+            ari = ar[b][1]
+            by_ari = terms[b][1]
+            nc.vector.scalar_tensor_tensor(
+                shaped(by_ari[:, 0, :], b), ari, -1.0, shaped(ae[b][:, 1, :], b), MULT, MULT
+            )
+            nc.vector.tensor_tensor(shaped(by_ari[:, 1, :], b), ari, shaped(ae[b][:, 0, :], b), MULT)
 
         def new_h(b):
-            return keep.tile([P, 2 * JB * PACK], BF16, name="h%d" % b, tag="h%d" % {5: 0, 6: 2, 7: 0}.get(b, b % 3), align_bytes=AL)
+            return keep.tile([P, 2 * R], BF16, name="h%d" % b, tag="h%d" % H_BUFFER[b], align_bytes=AL)
 
-        def combine_turned(b, first):
-            h = new_h(b)
-            for c in range(2):
-                acc = bank(first + c, [P, PACK, JB])
-                for n, term in enumerate(terms[b]):
+        def add_by_transposes(b, first):
+            h_b = new_h(b)
+            sums = [bank(first + c, [P, PACK, JB]) for c in range(2)]
+            by_arr, by_ari = terms[b]
+            for n, term in enumerate((by_ari, by_arr) if b < SHARED else (by_arr, by_ari)):
+                for c in range(2):
                     for t in range(PACK):
                         nc.tensor.matmul(
-                            out=acc[:, t, :], lhsT=term[:, c, t * P : (t + 1) * P], rhs=ident[:], is_transpose=True,
+                            out=sums[c][:, t, :], lhsT=term[:, c, t * P : (t + 1) * P], rhs=ident[:], is_transpose=True,
                             start=(n == 0 and t == 0), stop=(n == 1 and t == PACK - 1),
                         )
-                nc.scalar.copy(
-                    out=h[:, c * R : (c + 1) * R].rearrange("p (j t) -> p j t", t=PACK),
-                    in_=acc[:].rearrange("p t j -> p j t"),
-                )
-            return h
+                    if n == 1:
+                        nc.scalar.copy(
+                            out=h_b[:, c * R : (c + 1) * R].rearrange("p (j t) -> p j t", t=PACK),
+                            in_=sums[c][:].rearrange("p t j -> p j t"),
+                        )
+            return h_b
 
-        def flat(terms):
-            return terms.rearrange("p c x -> p (c x)")
-
-        def combine(b):
+        def add_on_gpsimd(b):
             by_arr, by_ari = terms[b]
-            h = new_h(b)
-            nc.gpsimd.tensor_tensor(h[:], flat(by_arr[:]), flat(by_ari[:]), ADD)
-            return h
+            h_b = new_h(b)
+            flat = "p c x -> p (c x)"
+            nc.gpsimd.tensor_tensor(h_b[:], by_arr[:].rearrange(flat), by_ari[:].rearrange(flat), ADD)
+            return h_b
+
+        def new_codes():
+            hq = ring.tile([P, 2 * JB], U32, name="hq", align_bytes=AL, bufs=3)
+            hq_sc = ring.tile([P, 2 * JB], U8, name="hq_sc", align_bytes=AL, bufs=3)
+            return hq, hq_sc
+
+        def new_scores():
+            return ring.tile([P, GROUPS, JB], F32, name="y_sb", bufs=4)
 
         def score_pass(y, g, part, hq, hq_sc):
             m = slice(g * P, (g + 1) * P)
             cols = slice(part * JB, (part + 1) * JB)
             if part == 0:
-                lhsT, lhsT_scale = nr[:, m].bitcast(FP8X4), n_sc8[4:P, m]
+                lhsT, lhsT_scale = nr[:, m].bitcast(FP8X4), n_sc8[ROW_NR:P, m]
             else:
                 lhsT, lhsT_scale = ni8[:, 2 * g * P : 2 * (g + 1) * P].bitcast(FP4X4), n_sc8[:, m]
             nc.tensor.matmul_mx(
@@ -243,15 +260,14 @@ def tile_list_ckg_none_kernel(
             rows = out[:, b * JB : (b + 1) * JB].rearrange("(g p) j -> p g j", p=P)
             queue.dma_start(out=rows[:, groups, :], in_=y_sb[:, groups, :])
 
-        def score(b, h):
-            hq = ring.tile([P, 2 * JB], U32, name="hq", align_bytes=AL, bufs=3)
-            hq_sc = ring.tile([P, 2 * JB], U8, name="hq_sc", align_bytes=AL, bufs=3)
-            nc.vector.quantize_mx(out=hq[:].bitcast(FP8X4), scales=hq_sc[:], in_=h[:])
-            tags = {BLOCKS - 3: [5, 4], BLOCKS - 2: [6, 7]}.get(b, [4 + b % 2])
-            per_bank = N // P // len(tags)
-            y_sb = ring.tile([P, N // P, JB], F32, name="y_sb", bufs=4)
-            for c, tag in enumerate(tags):
-                y = bank(tag, [P, per_bank, JB])
+        def score(b):
+            hq, hq_sc = new_codes()
+            nc.vector.quantize_mx(out=hq[:].bitcast(FP8X4), scales=hq_sc[:], in_=h[b][:])
+            banks = {LAST - 2: (SUMS + 1, SUMS), LAST - 1: (EVEN, EVEN + 1)}.get(b, (SUMS + b % 2,))
+            per_bank = GROUPS // len(banks)
+            y_sb = new_scores()
+            for c, number in enumerate(banks):
+                y = bank(number, [P, per_bank, JB])
                 groups = slice(c * per_bank, (c + 1) * per_bank)
                 for g in range(per_bank):
                     for part in range(2):
@@ -262,63 +278,54 @@ def tile_list_ckg_none_kernel(
         def last_block(b):
             arr, ari = ar[b]
             aer, aei = shaped(ae[b][:, 0, :], b), shaped(ae[b][:, 1, :], b)
-            by_arr = ring.tile([P, 2, R], F32, name="by_arr", bufs=4)
-            by_ari = ring.tile([P, 2, R], F32, name="by_ari", bufs=4)
+            by_arr, by_ari = new_terms()
             nc.vector.tensor_tensor(shaped(by_arr[:, 0, :], b), arr, aer, MULT)
             nc.vector.scalar_tensor_tensor(shaped(by_ari[:, 0, :], b), ari, -1.0, aei, MULT, MULT)
-            score(b - 3, h[b - 3])
-            score(b - 2, h[b - 2])
-            halves = [new_h(b)[:, 0:R], h[b - 1][:, 0:R]]
-            nc.gpsimd.tensor_tensor(halves[0], by_arr[:, 0, :], by_ari[:, 0, :], ADD)
+            score(b - 3)
+            score(b - 2)
+            hr, hi = new_h(b)[:, 0:R], h[b - 1][:, 0:R]
+            nc.gpsimd.tensor_tensor(hr, by_arr[:, 0, :], by_ari[:, 0, :], ADD)
             nc.vector.tensor_tensor(shaped(by_arr[:, 1, :], b), arr, aei, MULT)
             nc.vector.tensor_tensor(shaped(by_ari[:, 1, :], b), ari, aer, MULT)
-            score(b - 1, h[b - 1])
-            nc.vector.tensor_tensor(halves[1], by_arr[:, 1, :], by_ari[:, 1, :], ADD)
-            hq = ring.tile([P, 2 * JB], U32, name="hq", align_bytes=AL, bufs=3)
-            hq_sc = ring.tile([P, 2 * JB], U8, name="hq_sc", align_bytes=AL, bufs=3)
+            score(b - 1)
+            nc.vector.tensor_tensor(hi, by_arr[:, 1, :], by_ari[:, 1, :], ADD)
+            hq, hq_sc = new_codes()
+            for part, values in enumerate((hr, hi)):
+                cols = slice(part * JB, (part + 1) * JB)
+                nc.vector.quantize_mx(out=hq[:, cols].bitcast(FP8X4), scales=hq_sc[:, cols], in_=values)
+            banks = [bank(number, [P, JB]) for number in (ENTITY, ENTITY + 1, ODD, ODD + 1)]
             for part in range(2):
-                nc.vector.quantize_mx(
-                    out=hq[:, part * JB : (part + 1) * JB].bitcast(FP8X4),
-                    scales=hq_sc[:, part * JB : (part + 1) * JB],
-                    in_=halves[part],
-                )
-            banks = [bank(number, [P, JB]) for number in (0, 1, 2, 3)]
-            for part in range(2):
-                for g in range(N // P):
+                for g in range(GROUPS):
                     score_pass(banks[g][:], g, part, hq, hq_sc)
-            y_sb = ring.tile([P, N // P, JB], F32, name="y_sb", bufs=4)
-            for g in (0, 1):
+            y_sb = new_scores()
+            for g in range(0, GROUPS, 2):
                 nc.vector.tensor_copy(out=y_sb[:, g, :], in_=banks[g][:])
-            store(nc.sync, b, y_sb, slice(0, 2))
-            for g in (2, 3):
+            store(nc.sync, b, y_sb, slice(0, GROUPS, 2))
+            for g in range(1, GROUPS, 2):
                 nc.scalar.copy(out=y_sb[:, g, :], in_=banks[g][:])
-            store(nc.scalar, b, y_sb, slice(2, 4))
+            store(nc.scalar, b, y_sb, slice(1, GROUPS, 2))
 
         h, terms = {}, {}
-        after = {4: [0], 5: [2, 1], 6: [3]}
-        ae = {b: entity(b) for b in range(2)}
-        ar = {b: relation(b) for b in range(2)}
-        ae[2] = entity(2)
-        ar[2] = relation(2)
-        ae[3] = entity(3)
-        ar[3] = relation(3)
+        ae = {b: entity(b) for b in range(SHARED)}
+        ar = {b: relation(b) for b in range(SHARED)}
+        for b in range(SHARED, SHARED + 2):
+            ae[b] = entity(b)
+            ar[b] = relation(b)
         for b in range(SHARED):
-            for step in products(b):
-                step()
-        h[0] = combine_turned(0, 4)
-        for b in range(SHARED, BLOCKS - 1):
-            steps = products(b)
-            steps[0]()
-            for done in after.get(b, []):
-                score(done, h[done])
+            products_with_arr(b)
+            products_with_ari(b)
+        h[0] = add_by_transposes(0, SUMS)
+        for b in range(SHARED, LAST):
+            products_with_arr(b)
+            for done in QUANTISED_IN.get(b, ()):
+                score(done)
             if b > SHARED:
-                h[b - 1] = combine(b - 1)
-            steps[1]()
-            steps[2]()
+                h[b - 1] = add_on_gpsimd(b - 1)
+            products_with_ari(b)
             if b + 2 < BLOCKS:
                 ae[b + 2] = entity(b + 2)
                 ar[b + 2] = relation(b + 2)
             if b == SHARED:
-                h[1] = combine_turned(1, 4)
-        h[BLOCKS - 2] = combine_turned(BLOCKS - 2, 0)
-        last_block(BLOCKS - 1)
+                h[1] = add_by_transposes(1, SUMS)
+        h[LAST - 1] = add_by_transposes(LAST - 1, ENTITY)
+        last_block(LAST)

@@ -79,18 +79,17 @@ def tile_list_ckg_none_kernel(
             for s in range(4):
                 queue.dma_start(out=plane[first + s : P : 32, :], in_=rows[s])
 
-        for plane in (tab_e_sc, we_sc_raw, tab_r_sc, n_sc):
+        for plane in (tab_e_sc, tab_r_sc, we_sc_raw, n_sc):
             nc.vector.memset(plane[:], 0)
-        nc.vector.memset(ident[:], 0.0)
-        load_scales(nc.gpsimd, we_sc_raw, wei_scales, ROW_WEI)
-        make_identity(nc, ident[:], nomemset=True)
+        make_identity(nc, ident[:])
         nc.sync.dma_start(list_e[:], offs)
-        nc.sync.dma_start(list_r[:], offs2)
         nc.sync.dma_start(out=tab_e[:, 0:FRONT], in_=words(tab_words)[:, 0:FRONT])
         load_scales(nc.sync, tab_e_sc, tab_scales, 0)
         nc.sync.dma_start(out=tab_e[:, FRONT:T], in_=words(tab_words)[:, FRONT:T])
-        nc.sync.dma_start(out=wr_raw[0][:], in_=wrr.rearrange("(p i) r -> p i r", i=PACK))
+        nc.sync.dma_start(list_r[:], offs2)
         load_scales(nc.sync, tab_r_sc, tab2_scales, ROW_V2)
+        nc.sync.dma_start(out=wr_raw[0][:], in_=wrr.rearrange("(p i) r -> p i r", i=PACK))
+        load_scales(nc.sync, we_sc_raw, wei_scales, ROW_WEI)
         nc.sync.dma_start(out=wr_raw[1][:], in_=wri.rearrange("(p i) r -> p i r", i=PACK))
         nc.sync.dma_start(out=we_raw[:, 0, :], in_=words(wer_words))
         nc.sync.dma_start(out=we_raw[:, 1, :], in_=words(wei_words))

@@ -28,6 +28,7 @@ FRONT = 768
 SHARED = 2
 PIECE = SHARED * JB
 TURNED = (0, 1, LAST - 1)
+SHORT = 384
 
 ROW_WER, ROW_WEI, ROW_V2, ROW_NR = 4, 8, 12, 4
 
@@ -243,9 +244,9 @@ def tile_list_ckg_none_kernel(
         def new_scores():
             return ring.tile([P, GROUPS, JB], F32, name="y_sb", bufs=4)
 
-        def score_pass(y, g, part, hq, hq_sc):
+        def score_pass(y, g, part, hq, hq_sc, width=JB):
             m = slice(g * P, (g + 1) * P)
-            cols = slice(part * JB, (part + 1) * JB)
+            cols = slice(part * width, (part + 1) * width)
             if part == 0:
                 lhsT, lhsT_scale = nr[:, m].bitcast(FP8X4), n_sc8[ROW_NR:P, m]
             else:
@@ -274,18 +275,37 @@ def tile_list_ckg_none_kernel(
                 nc.scalar.copy(out=y_sb[:, groups, :], in_=y[:])
                 store(nc.sync, b, y_sb, groups)
 
+        def score_pair(b):
+            hq = keep.tile([P, 4 * JB], U32, name="hq_pair", align_bytes=AL)
+            hq_sc = keep.tile([P, 4 * JB], U8, name="hq_pair_sc", align_bytes=AL)
+            for k in range(2):
+                for part in range(2):
+                    cols = slice((2 * part + k) * JB, (2 * part + k + 1) * JB)
+                    nc.vector.quantize_mx(
+                        out=hq[:, cols].bitcast(FP8X4), scales=hq_sc[:, cols], in_=h[b + k][:, part * R : (part + 1) * R]
+                    )
+            y_sb = keep.tile([P, GROUPS, 2 * JB], F32, name="y_pair")
+            rows = out[:, b * JB : (b + 2) * JB].rearrange("(g p) j -> p g j", p=P)
+            for c in range(2):
+                y = bank(SUMS + c, [P, 2, 2 * JB])
+                for g in range(2):
+                    for part in range(2):
+                        score_pass(y[:, g, :], 2 * c + g, part, hq, hq_sc, 2 * JB)
+                nc.scalar.copy(out=y_sb[:, 2 * c : 2 * c + 2, :], in_=y[:])
+                nc.sync.dma_start(out=rows[:, 2 * c : 2 * c + 2, :], in_=y_sb[:, 2 * c : 2 * c + 2, :])
+
         def last_block(b):
             arr, ari = ar[b]
             aer, aei = shaped(ae[b][:, 0, :], b), shaped(ae[b][:, 1, :], b)
             by_arr, by_ari = new_terms()
             nc.vector.tensor_tensor(shaped(by_arr[:, 0, :], b), arr, aer, MULT)
             nc.vector.scalar_tensor_tensor(shaped(by_ari[:, 0, :], b), ari, -1.0, aei, MULT, MULT)
-            score(b - 3)
-            score(b - 2)
+            score_pair(b - 3)
             hr, hi = new_h(b)[:, 0:R], h[b - 1][:, 0:R]
-            nc.gpsimd.tensor_tensor(hr, by_arr[:, 0, :], by_ari[:, 0, :], ADD)
+            nc.gpsimd.tensor_tensor(hr[:, 0:SHORT], by_arr[:, 0, 0:SHORT], by_ari[:, 0, 0:SHORT], ADD)
             nc.vector.tensor_tensor(shaped(by_arr[:, 1, :], b), arr, aei, MULT)
             nc.vector.tensor_tensor(shaped(by_ari[:, 1, :], b), ari, aer, MULT)
+            nc.vector.tensor_tensor(hr[:, SHORT:R], by_arr[:, 0, SHORT:R], by_ari[:, 0, SHORT:R], ADD)
             score(b - 1)
             nc.vector.tensor_tensor(hi, by_arr[:, 1, :], by_ari[:, 1, :], ADD)
             hq, hq_sc = new_codes()

@@ -260,10 +260,14 @@ def tile_list_ckg_none_kernel(
             rows = out[:, b * JB : (b + 1) * JB].rearrange("(g p) j -> p g j", p=P)
             queue.dma_start(out=rows[:, groups, :], in_=y_sb[:, groups, :])
 
-        def score(b):
+        def quantise(b):
             hq, hq_sc = new_codes()
             nc.vector.quantize_mx(out=hq[:].bitcast(FP8X4), scales=hq_sc[:], in_=h[b][:])
-            banks = {LAST - 2: (SUMS + 1, SUMS), LAST - 1: (EVEN, EVEN + 1)}.get(b, (SUMS + b % 2,))
+            return hq, hq_sc
+
+        def score(b, codes=None):
+            hq, hq_sc = codes or quantise(b)
+            banks = {1: (EVEN,), 3: (EVEN + 1,), LAST - 1: (EVEN, EVEN + 1)}.get(b, (SUMS + b % 2,))
             per_bank = GROUPS // len(banks)
             y_sb = new_scores()
             for c, number in enumerate(banks):
@@ -324,7 +328,7 @@ def tile_list_ckg_none_kernel(
                 nc.scalar.copy(out=y_sb[:, g, :], in_=banks[g][:])
             store(nc.scalar, b, y_sb, slice(1, GROUPS, 2))
 
-        h, terms = {}, {}
+        h, terms, held = {}, {}, {}
         ae = {b: entity(b) for b in range(SHARED)}
         ar = {b: relation(b) for b in range(SHARED)}
         for b in range(SHARED, SHARED + 2):
@@ -337,7 +341,12 @@ def tile_list_ckg_none_kernel(
         for b in range(SHARED, LAST):
             products_with_arr(b)
             for done in QUANTISED_IN.get(b, ()):
-                score(done)
+                if done in (1, 3):
+                    held[done] = quantise(done)
+                else:
+                    score(done)
+            if b == LAST - 1:
+                score(1, held[1])
             if b > SHARED:
                 h[b - 1] = add_on_gpsimd(b - 1)
             products_with_ari(b)
@@ -347,4 +356,5 @@ def tile_list_ckg_none_kernel(
             if b == SHARED:
                 h[1] = add_by_transposes(1, SUMS)
         h[LAST - 1] = add_by_transposes(LAST - 1, ENTITY)
+        score(3, held[3])
         last_block(LAST)

@@ -34,7 +34,7 @@ ROW_WER, ROW_WEI, ROW_V2, ROW_NR = 4, 8, 12, 4
 
 ENTITY, ODD, SUMS, EVEN = 0, 2, 4, 6
 
-QUANTISED_IN = {4: (0,), 5: (2, 1), 6: (3,)}
+QUANTISED_IN = {5: (2, 1), 6: (3,)}
 H_BUFFER = (0, 1, 2, 0, 1, 0, 2, 0)
 
 
@@ -186,11 +186,14 @@ def tile_list_ckg_none_kernel(
             by_ari = ring.tile([P, 2, R], F32, name="by_ari", bufs=4)
             return by_arr, by_ari
 
-        def products_with_arr(b):
+        def products_with_arr(b, part=None):
             arr = ar[b][0]
-            terms[b] = new_terms()
+            if b not in terms:
+                terms[b] = new_terms()
             by_arr = terms[b][0]
-            if b in TURNED:
+            if part is not None:
+                nc.vector.tensor_tensor(shaped(by_arr[:, part, :], b), arr, shaped(ae[b][:, part, :], b), MULT)
+            elif b in TURNED:
                 engine = nc.gpsimd if b < SHARED else nc.vector
                 engine.tensor_tensor(by_arr[:], arr.unsqueeze(1).to_broadcast([P, 2, R]), ae[b][:], MULT)
             else:
@@ -339,17 +342,21 @@ def tile_list_ckg_none_kernel(
             products_with_ari(b)
         h[0] = add_by_transposes(0, SUMS)
         for b in range(SHARED, LAST):
-            products_with_arr(b)
-            for done in QUANTISED_IN.get(b, ()):
-                if done in (1, 3):
+            if b in QUANTISED_IN:
+                products_with_arr(b, 0)
+                for done in QUANTISED_IN[b]:
                     held[done] = quantise(done)
-                else:
-                    score(done)
-            if b == LAST - 1:
-                score(1, held[1])
-            if b > SHARED:
+                h[b - 1] = add_on_gpsimd(b - 1)
+                products_with_arr(b, 1)
+                score(b - 3 if b < LAST - 1 else 1, held[b - 3 if b < LAST - 1 else 1])
+            else:
+                products_with_arr(b)
+            if b == SHARED + 1:
                 h[b - 1] = add_on_gpsimd(b - 1)
             products_with_ari(b)
+            if b == SHARED + 1:
+                score(0)
+                h[b] = add_on_gpsimd(b)
             if b + 2 < BLOCKS:
                 ae[b + 2] = entity(b + 2)
                 ar[b + 2] = relation(b + 2)

from contextlib import ExitStack

import concourse.mybir as mybir
from concourse.masks import make_identity

K, L, R, N, T, J = 512, 512, 512, 512, 2048, 1024
FLOPS = 2 * J * (2 * K * R + 2 * L * R + 2 * R * N)

F32 = mybir.dt.float32
BF16 = mybir.dt.bfloat16
I32 = mybir.dt.int32
U32 = mybir.dt.uint32
U16 = mybir.dt.uint16
U8 = mybir.dt.uint8
FP8X4 = mybir.dt.float8_e4m3fn_x4
FP4X4 = mybir.dt.float4_e2m1fn_x4
MULT = mybir.AluOpType.mult
ADD = mybir.AluOpType.add

P = 128
PACK = 4
JB = 128
BLOCKS = J // JB
LAST = BLOCKS - 1
GROUPS = N // P
AL = 64
FRONT = 768
SHARED = 2
PIECE = SHARED * JB
TURNED = (0, 1, LAST - 1)
SHORT = 384

ROW_WER, ROW_WEI, ROW_V2, ROW_NR = 4, 8, 12, 4

ENTITY, ODD, SUMS, EVEN = 0, 2, 4, 6

QUANTISED_IN = {5: (2, 1), 6: (3,)}
H_BUFFER = (0, 1, 2, 0, 1, 0, 2, 0)


def tile_list_ckg_none_kernel(
    tc, tab_words, tab_scales, tab2_words, tab2_scales, wer_words, wer_scales, wei_words, wei_scales,
    wrr, wri, nr_words, nr_scales, ni_words, ni_scales, offs, offs2, out,
):
    nc = tc.nc
    with ExitStack() as ctx:
        keep = ctx.enter_context(tc.tile_pool(name="keep", bufs=1))
        ring = ctx.enter_context(tc.tile_pool(name="ring", bufs=SHARED))
        psum = ctx.enter_context(tc.psum_pool(name="psum", bufs=1))

        list_e = keep.tile([P, J // 16], U16, name="list_e")
        list_r = keep.tile([P, J // 16], U16, name="list_r")
        tab_e = keep.tile([P, T], I32, name="tab_e", align_bytes=AL)
        tab_r = keep.tile([P, T], I32, name="tab_r", align_bytes=AL)
        tab_e_sc = keep.tile([P, T // 4], I32, name="tab_e_sc", align_bytes=AL)
        tab_r_sc = keep.tile([P, T // 4], I32, name="tab_r_sc", align_bytes=AL)
        we_raw = keep.tile([P, 2, R], I32, name="we_raw", align_bytes=AL)
        we_sc_raw = keep.tile([P, R // 4], I32, name="we_sc_raw", align_bytes=AL)
        we_sc = keep.tile([P, R], U8, name="we_sc", align_bytes=AL)
        wr_raw = [keep.tile([P, PACK, R], F32, name="wr_raw%d" % c, align_bytes=AL) for c in range(2)]
        wr_bf = [keep.tile([P, R * PACK], BF16, name="wr_bf%d" % c, align_bytes=AL) for c in range(2)]
        n_sc = keep.tile([P, N // 4], I32, name="n_sc", align_bytes=AL)
        nr = keep.tile([P, N], I32, name="nr", align_bytes=AL)
        ni = keep.tile([P, N // 2], I32, name="ni", align_bytes=AL)
        ve = keep.tile([P, J], U32, name="ve", align_bytes=AL)
        ve_sc = keep.tile([P, J], U8, name="ve_sc", align_bytes=AL)
        vr_sc = keep.tile([P, J], U8, name="vr_sc", align_bytes=AL)
        vr = keep.tile([P, J], U32, name="vr", align_bytes=AL)
        we = keep.tile([P, 2, R], I32, name="we", align_bytes=AL)
        ident = keep.tile([P, P], F32, name="ident", align_bytes=AL)

        def bank(number, shape):
            return psum.tile(shape, F32, name="bank%d" % number, tag="bank%d" % number)

        def words(ap):
            return ap[0].rearrange("p n i -> p (n i)").bitcast(I32)

        def load_scales(queue, plane, scales, first):
            rows = scales[0].bitcast(I32).rearrange("(q s) c -> s q c", s=4)
            for s in range(4):
                queue.dma_start(out=plane[first + s : P : 32, :], in_=rows[s])

        for plane in (tab_e_sc, tab_r_sc, we_sc_raw, n_sc):
            nc.vector.memset(plane[:], 0)
        make_identity(nc, ident[:])
        nc.sync.dma_start(list_e[:], offs)
        nc.sync.dma_start(out=tab_e[:, 0:FRONT], in_=words(tab_words)[:, 0:FRONT])
        load_scales(nc.sync, tab_e_sc, tab_scales, 0)
        nc.sync.dma_start(out=tab_e[:, FRONT:T], in_=words(tab_words)[:, FRONT:T])
        nc.sync.dma_start(list_r[:], offs2)
        load_scales(nc.sync, tab_r_sc, tab2_scales, ROW_V2)
        nc.sync.dma_start(out=wr_raw[0][:], in_=wrr.rearrange("(p i) r -> p i r", i=PACK))
        load_scales(nc.sync, we_sc_raw, wei_scales, ROW_WEI)
        nc.sync.dma_start(out=wr_raw[1][:], in_=wri.rearrange("(p i) r -> p i r", i=PACK))
        nc.sync.dma_start(out=we_raw[:, 0, :], in_=words(wer_words))
        nc.sync.dma_start(out=we_raw[:, 1, :], in_=words(wei_words))
        load_scales(nc.sync, we_sc_raw, wer_scales, ROW_WER)
        nc.sync.dma_start(out=tab_r[:], in_=words(tab2_words))
        nc.sync.dma_start(out=nr[:], in_=words(nr_words))
        nc.sync.dma_start(out=ni[:], in_=ni_words[0].bitcast(I32))
        load_scales(nc.sync, n_sc, ni_scales, 0)
        load_scales(nc.sync, n_sc, nr_scales, ROW_NR)

        def gather(dst, window, offsets, first, last):
            nc.vector.tensor_copy(dst[:, first:last], window.indirect(offsets[:, first // 16 : last // 16]))

        gather(ve_sc, tab_e_sc[:].bitcast(U8), list_e, 0, J)
        gather(ve, tab_e[:].bitcast(U32), list_e, 0, J)
        gather(vr_sc, tab_r_sc[:].bitcast(U8), list_r, 0, J)

        for c in range(2):
            nc.scalar.copy(
                out=wr_bf[c][:].rearrange("p (t m i) -> p m i t", t=PACK, i=PACK),
                in_=wr_raw[c][:].rearrange("p i (m t) -> p m i t", t=PACK),
            )
        for c in range(2):
            nc.vector.tensor_copy(
                out=we[:, c, :].rearrange("p (t m) -> p m t", t=PACK),
                in_=we_raw[:, c, :].rearrange("p (m t) -> p m t", t=PACK),
            )
        nc.vector.tensor_copy(
            out=we_sc[:].rearrange("p (t m) -> p t m", t=PACK),
            in_=we_sc_raw[:].bitcast(U8).rearrange("p (m t) -> p t m", t=PACK),
        )
        wr_sc = keep.tile([P, 2, R], U8, name="wr_sc", tag="we_sc_raw", align_bytes=AL)
        wr = [we_raw[:, 0, :], we_raw[:, 1, :]]
        for c in range(2):
            nc.vector.quantize_mx(out=wr[c].bitcast(FP8X4), scales=wr_sc[:, c, :], in_=wr_bf[c][:])
        gather(vr, tab_r[:].bitcast(U32), list_r, 0, PIECE)
        gather(vr, tab_r[:].bitcast(U32), list_r, PIECE, J)
        n_sc8 = n_sc[:].bitcast(U8)
        ni8 = ni[:].bitcast(U8)

        weights = [
            (we[:, 0, :], we_sc[ROW_WER:P, :]),
            (we[:, 1, :], we_sc[ROW_WEI:P, :]),
            (wr[0], wr_sc[:, 0, :]),
            (wr[1], wr_sc[:, 1, :]),
        ]
        picked = [(ve, ve_sc[:, :]), (ve, ve_sc[:, :]), (vr, vr_sc[ROW_V2:P, :]), (vr, vr_sc[ROW_V2:P, :])]

        def project(number, which, b):
            codes, plane = weights[which]
            columns, columns_sc = picked[which]
            cols = slice(b * JB, (b + 1) * JB)
            if b in TURNED:
                acc = bank(number, [P, R])
                nc.tensor.matmul_mx(
                    out=acc[:], lhsT=columns[:, cols].bitcast(FP8X4), lhsT_scale=columns_sc[:, cols],
                    rhs=codes.bitcast(FP8X4), rhs_scale=plane, start=True, stop=True,
                )
                return acc[:]
            acc = bank(number, [P, PACK, JB])
            for t in range(PACK):
                m = slice(t * P, (t + 1) * P)
                nc.tensor.matmul_mx(
                    out=acc[:, t, :], lhsT=codes[:, m].bitcast(FP8X4), lhsT_scale=plane[:, m],
                    rhs=columns[:, cols].bitcast(FP8X4), rhs_scale=columns_sc[:, cols], start=True, stop=True,
                )
            return acc[:].rearrange("p t j -> p j t")

        def shaped(row, b):
            if b in TURNED:
                return row
            return row.rearrange("p (j t) -> p j t", t=PACK)

        def entity(b):
            first = {0: ODD, 1: EVEN}.get(b, ENTITY)
            both = ring.tile([P, 2, R], F32, name="ae", bufs=4)
            for c in range(2):
                nc.scalar.copy(out=shaped(both[:, c, :], b), in_=project(first + c, c, b))
            return both

        def relation(b):
            first = ODD if b % 2 else EVEN
            banks = (ENTITY + b, SUMS + b) if b < SHARED else (first, first + 1)
            arr = project(banks[0], 2, b)
            if b < SHARED:
                arr_sb = ring.tile([P, R], F32, name="arr_sb")
                nc.scalar.copy(out=arr_sb[:], in_=arr)
                arr = arr_sb[:]
            return arr, project(banks[1], 3, b)

        def new_terms():
            by_arr = ring.tile([P, 2, R], F32, name="by_arr", bufs=4)
            by_ari = ring.tile([P, 2, R], F32, name="by_ari", bufs=4)
            return by_arr, by_ari

        def products_with_arr(b, part=None):
            arr = ar[b][0]
            if b not in terms:
                terms[b] = new_terms()
            by_arr = terms[b][0]
            if part is not None:
                nc.vector.tensor_tensor(shaped(by_arr[:, part, :], b), arr, shaped(ae[b][:, part, :], b), MULT)
            elif b in TURNED:
                engine = nc.gpsimd if b < SHARED else nc.vector
                engine.tensor_tensor(by_arr[:], arr.unsqueeze(1).to_broadcast([P, 2, R]), ae[b][:], MULT)
            else:
                split = "p c (j t) -> p c j t"
                nc.vector.tensor_tensor(
                    by_arr[:].rearrange(split, t=PACK), arr.unsqueeze(1).to_broadcast([P, 2, JB, PACK]),
                    ae[b][:].rearrange(split, t=PACK), MULT,
                )

        def products_with_ari(b):
            ari = ar[b][1]
            by_ari = terms[b][1]
            nc.vector.scalar_tensor_tensor(
                shaped(by_ari[:, 0, :], b), ari, -1.0, shaped(ae[b][:, 1, :], b), MULT, MULT
            )
            nc.vector.tensor_tensor(shaped(by_ari[:, 1, :], b), ari, shaped(ae[b][:, 0, :], b), MULT)

        def new_h(b):
            return keep.tile([P, 2 * R], BF16, name="h%d" % b, tag="h%d" % H_BUFFER[b], align_bytes=AL)

        def add_by_transposes(b, first):
            h_b = new_h(b)
            sums = [bank(first + c, [P, PACK, JB]) for c in range(2)]
            by_arr, by_ari = terms[b]
            for n, term in enumerate((by_ari, by_arr) if b < SHARED else (by_arr, by_ari)):
                for c in range(2):
                    for t in range(PACK):
                        nc.tensor.matmul(
                            out=sums[c][:, t, :], lhsT=term[:, c, t * P : (t + 1) * P], rhs=ident[:], is_transpose=True,
                            start=(n == 0 and t == 0), stop=(n == 1 and t == PACK - 1),
                        )
                    if n == 1:
                        nc.scalar.copy(
                            out=h_b[:, c * R : (c + 1) * R].rearrange("p (j t) -> p j t", t=PACK),
                            in_=sums[c][:].rearrange("p t j -> p j t"),
                        )
            return h_b

        def add_on_gpsimd(b):
            by_arr, by_ari = terms[b]
            h_b = new_h(b)
            flat = "p c x -> p (c x)"
            nc.gpsimd.tensor_tensor(h_b[:], by_arr[:].rearrange(flat), by_ari[:].rearrange(flat), ADD)
            return h_b

        def new_codes():
            hq = ring.tile([P, 2 * JB], U32, name="hq", align_bytes=AL, bufs=3)
            hq_sc = ring.tile([P, 2 * JB], U8, name="hq_sc", align_bytes=AL, bufs=3)
            return hq, hq_sc

        def new_scores():
            return ring.tile([P, GROUPS, JB], F32, name="y_sb", bufs=4)

        def score_pass(y, g, part, hq, hq_sc, width=JB):
            m = slice(g * P, (g + 1) * P)
            cols = slice(part * width, (part + 1) * width)
            if part == 0:
                lhsT, lhsT_scale = nr[:, m].bitcast(FP8X4), n_sc8[ROW_NR:P, m]
            else:
                lhsT, lhsT_scale = ni8[:, 2 * g * P : 2 * (g + 1) * P].bitcast(FP4X4), n_sc8[:, m]
            nc.tensor.matmul_mx(
                out=y, lhsT=lhsT, lhsT_scale=lhsT_scale, rhs=hq[:, cols].bitcast(FP8X4), rhs_scale=hq_sc[:, cols],
                start=(part == 0), stop=(part == 1),
            )

        def store(queue, b, y_sb, groups):
            rows = out[:, b * JB : (b + 1) * JB].rearrange("(g p) j -> p g j", p=P)
            queue.dma_start(out=rows[:, groups, :], in_=y_sb[:, groups, :])

        def quantise(b):
            hq, hq_sc = new_codes()
            nc.vector.quantize_mx(out=hq[:].bitcast(FP8X4), scales=hq_sc[:], in_=h[b][:])
            return hq, hq_sc

        def score(b, codes=None):
            hq, hq_sc = codes or quantise(b)
            banks = {1: (EVEN,), 3: (EVEN + 1,), LAST - 1: (EVEN, EVEN + 1)}.get(b, (SUMS + b % 2,))
            per_bank = GROUPS // len(banks)
            y_sb = new_scores()
            for c, number in enumerate(banks):
                y = bank(number, [P, per_bank, JB])
                groups = slice(c * per_bank, (c + 1) * per_bank)
                for g in range(per_bank):
                    for part in range(2):
                        score_pass(y[:, g, :], groups.start + g, part, hq, hq_sc)
                nc.scalar.copy(out=y_sb[:, groups, :], in_=y[:])
                store(nc.sync, b, y_sb, groups)

        def score_pair(b):
            hq = keep.tile([P, 4 * JB], U32, name="hq_pair", align_bytes=AL)
            hq_sc = keep.tile([P, 4 * JB], U8, name="hq_pair_sc", align_bytes=AL)
            for k in range(2):
                for part in range(2):
                    cols = slice((2 * part + k) * JB, (2 * part + k + 1) * JB)
                    nc.vector.quantize_mx(
                        out=hq[:, cols].bitcast(FP8X4), scales=hq_sc[:, cols], in_=h[b + k][:, part * R : (part + 1) * R]
                    )
            y_sb = keep.tile([P, GROUPS, 2 * JB], F32, name="y_pair")
            rows = out[:, b * JB : (b + 2) * JB].rearrange("(g p) j -> p g j", p=P)
            for c in range(2):
                y = bank(SUMS + c, [P, 2, 2 * JB])
                for g in range(2):
                    for part in range(2):
                        score_pass(y[:, g, :], 2 * c + g, part, hq, hq_sc, 2 * JB)
                nc.scalar.copy(out=y_sb[:, 2 * c : 2 * c + 2, :], in_=y[:])
                nc.sync.dma_start(out=rows[:, 2 * c : 2 * c + 2, :], in_=y_sb[:, 2 * c : 2 * c + 2, :])

        def last_block(b):
            arr, ari = ar[b]
            aer, aei = shaped(ae[b][:, 0, :], b), shaped(ae[b][:, 1, :], b)
            by_arr, by_ari = new_terms()
            nc.vector.tensor_tensor(shaped(by_arr[:, 0, :], b), arr, aer, MULT)
            nc.vector.scalar_tensor_tensor(shaped(by_ari[:, 0, :], b), ari, -1.0, aei, MULT, MULT)
            score_pair(b - 3)
            hr, hi = new_h(b)[:, 0:R], h[b - 1][:, 0:R]
            nc.gpsimd.tensor_tensor(hr[:, 0:SHORT], by_arr[:, 0, 0:SHORT], by_ari[:, 0, 0:SHORT], ADD)
            nc.vector.tensor_tensor(shaped(by_arr[:, 1, :], b), arr, aei, MULT)
            nc.vector.tensor_tensor(shaped(by_ari[:, 1, :], b), ari, aer, MULT)
            nc.vector.tensor_tensor(hr[:, SHORT:R], by_arr[:, 0, SHORT:R], by_ari[:, 0, SHORT:R], ADD)
            score(b - 1)
            nc.vector.tensor_tensor(hi, by_arr[:, 1, :], by_ari[:, 1, :], ADD)
            hq, hq_sc = new_codes()
            for part, values in enumerate((hr, hi)):
                cols = slice(part * JB, (part + 1) * JB)
                nc.vector.quantize_mx(out=hq[:, cols].bitcast(FP8X4), scales=hq_sc[:, cols], in_=values)
            banks = [bank(number, [P, JB]) for number in (ENTITY, ENTITY + 1, ODD, ODD + 1)]
            for part in range(2):
                for g in range(GROUPS):
                    score_pass(banks[g][:], g, part, hq, hq_sc)
            y_sb = new_scores()
            for g in range(0, GROUPS, 2):
                nc.vector.tensor_copy(out=y_sb[:, g, :], in_=banks[g][:])
            store(nc.sync, b, y_sb, slice(0, GROUPS, 2))
            for g in range(1, GROUPS, 2):
                nc.scalar.copy(out=y_sb[:, g, :], in_=banks[g][:])
            store(nc.scalar, b, y_sb, slice(1, GROUPS, 2))

        h, terms, held = {}, {}, {}
        ae = {b: entity(b) for b in range(SHARED)}
        ar = {b: relation(b) for b in range(SHARED)}
        for b in range(SHARED, SHARED + 2):
            ae[b] = entity(b)
            ar[b] = relation(b)
        for b in range(SHARED):
            products_with_arr(b)
            products_with_ari(b)
        h[0] = add_by_transposes(0, SUMS)
        for b in range(SHARED, LAST):
            if b in QUANTISED_IN:
                products_with_arr(b, 0)
                for done in QUANTISED_IN[b]:
                    held[done] = quantise(done)
                h[b - 1] = add_on_gpsimd(b - 1)
                products_with_arr(b, 1)
                score(b - 3 if b < LAST - 1 else 1, held[b - 3 if b < LAST - 1 else 1])
            else:
                products_with_arr(b)
            if b == SHARED + 1:
                h[b - 1] = add_on_gpsimd(b - 1)
            products_with_ari(b)
            if b == SHARED + 1:
                score(0)
                h[b] = add_on_gpsimd(b)
            if b + 2 < BLOCKS:
                ae[b + 2] = entity(b + 2)
                ar[b + 2] = relation(b + 2)
            if b == SHARED:
                h[1] = add_by_transposes(1, SUMS)
        h[LAST - 1] = add_by_transposes(LAST - 1, ENTITY)
        score(3, held[3])
        last_block(LAST)
